import numpy as np
import ml_dtypes


def mxq(x, axis, fmt="e4m3"):
    dtype, down = {"e4m3": (ml_dtypes.float8_e4m3fn, 7), "e5m2": (ml_dtypes.float8_e5m2, 14)}[fmt]
    v = np.moveaxis(np.asarray(x, np.float32).astype(ml_dtypes.bfloat16).astype(np.float64), axis, -1)
    blocks = v.reshape(v.shape[:-1] + (-1, 32))
    amax = np.abs(blocks).max(-1, keepdims=True)
    byte = np.maximum(np.where(amax > 0, np.frexp(amax)[1] - 1 + 127, 0) - down, 1)
    scale = np.exp2(byte - 127.0)
    codes = (blocks / scale).astype(np.float32).astype(dtype).astype(np.float64)
    return np.moveaxis((codes * scale).reshape(v.shape), -1, axis)


WIDE = False


def mx_kscale(k):
    if not WIDE:
        return np.ones(k)
    levels = np.array([10, -10, 5, -5, 0])
    if k % 512:
        return np.exp2(np.random.permutation(np.resize(levels, k // 32))).repeat(32)
    a = np.empty((k // 512, 16))
    for p in range(k // 512):
        a[p, :8] = np.random.permutation(np.resize(levels, 8))
        for g in range(8):
            far = levels[np.abs(levels - a[p, g]) >= 10]
            a[p, g + 8] = far[np.random.randint(len(far))]
    return np.exp2(a.ravel()).repeat(32)


BF16 = ml_dtypes.bfloat16


def bf(x):
    return np.asarray(x, np.float32).astype(BF16)


def f64(x):
    return np.asarray(x).astype(np.float64)


E2M1 = np.array([0.0, 0.5, 1.0, 1.5, 2.0, 3.0, 4.0, 6.0, -0.0, -0.5, -1.0, -1.5, -2.0, -3.0, -4.0, -6.0])


def pack_weight(w, fmt):
    k, n = w.shape
    w = f64(bf(w)).reshape(k // 32, 32, n)
    amax = np.abs(w).max(1)
    if fmt == "e4m3":
        byte = np.frexp(amax)[1] - 1 + 127 - 7
    else:
        mant, ex = np.frexp(amax / 6.0)
        byte = np.where(mant > 0.5, ex, ex - 1) + 127
    byte = np.clip(np.where(amax > 0, byte, 1), 1, 254)
    scaled = (w * np.exp2(127.0 - byte)[:, None, :]).reshape(k, n).astype(np.float32)
    by_word = np.ascontiguousarray(scaled.reshape(k // 512, 128, 4, n).transpose(0, 1, 3, 2))
    if fmt == "e4m3":
        words = by_word.astype(ml_dtypes.float8_e4m3fn).view(np.uint8)
    else:
        c = by_word.astype(ml_dtypes.float4_e2m1fn).view(np.uint8) & 0xF
        words = c[..., 0::2] | (c[..., 1::2] << 4)
    return np.ascontiguousarray(words), np.ascontiguousarray(byte.astype(np.uint8).reshape(k // 512, 16, n))


def unpack_weight(words, scales, fmt):
    g, p, n, _ = words.shape
    if fmt == "e4m3":
        vals = np.ascontiguousarray(words).view(ml_dtypes.float8_e4m3fn).astype(np.float64)
    else:
        nib = np.empty((g, p, n, 4), np.uint8)
        nib[..., 0::2] = words & 0xF
        nib[..., 1::2] = words >> 4
        vals = E2M1[nib]
    vals = vals * np.repeat(np.exp2(scales.astype(np.float64) - 127.0), 8, axis=1)[..., None]
    return vals.transpose(0, 1, 3, 2).reshape(g * 512, n)
def pack4(w):
    words, scales = pack_weight(w, "e2m1")
    return words.reshape(words.shape[0], 128, -1), scales


def unpack4(words, scales):
    return unpack_weight(words.reshape(words.shape[0], 128, -1, 2), scales, "e2m1")


M, N, H, D = 1024, 1536, 2, 512
C = H * D


def relative_bias():
    lag = np.arange(M + N - 1) - (M - 1)
    table = np.random.standard_normal((H, M + N - 1)) - np.arange(1, H + 1)[:, None] * np.abs(lag)[None, :] / N
    index = np.arange(N)[None, :] - np.arange(M)[:, None] + (M - 1)
    return table[:, index]


def draw0():
    s, t = mx_kscale(C), mx_kscale(N)
    keys_words, keys_scales = pack4(1.3 * np.random.standard_normal((C, N)) / np.sqrt(D) / s[:, None])
    values_words, values_scales = pack4(4.0 * np.random.standard_normal((N, C)) / t[:, None])
    gate_words, gate_scales = pack4(np.random.standard_normal((C, C)) / np.sqrt(C) / s[:, None])
    return {"x": bf(np.random.standard_normal((M, C)) * s),
            "keys_words": keys_words,
            "keys_scales": keys_scales,
            "rel_bias": bf(relative_bias()),
            "anchor_gain": bf((1.0 + 0.1 * np.random.standard_normal((H, N))) * t),
            "values_words": values_words,
            "values_scales": values_scales,
            "gate_words": gate_words,
            "gate_scales": gate_scales,
            "gate_bias": bf(0.5 * np.random.standard_normal(C))}


def core(x, keys_words, keys_scales, rel_bias, anchor_gain, values_words, values_scales, gate_words, gate_scales, gate_bias):
    xq = mxq(f64(x), 1, "e4m3")
    keys = unpack4(keys_words, keys_scales)
    values = unpack4(values_words, values_scales)
    gate = unpack4(gate_words, gate_scales)
    bias = f64(rel_bias)
    gain = f64(anchor_gain)
    heads = []
    for h in range(H):
        score = (xq[:, h * D:(h + 1) * D] @ keys[h * D:(h + 1) * D, :]) + bias[h]
        e = np.exp(score - np.max(score, axis=1, keepdims=True))
        num = mxq(e * gain[h], 1, "e4m3") @ values[:, h * D:(h + 1) * D]
        heads.append(num / np.sum(e, axis=1, keepdims=True))
    attended = np.concatenate(heads, axis=1)
    z = (xq @ gate) + f64(gate_bias)
    return attended / (1.0 + np.exp(-z))


def e4m3fn_bytes(y):
    return np.clip(np.asarray(y, np.float64), -448.0, 448.0).astype(np.float32).astype(ml_dtypes.float8_e4m3fn).view(np.uint8)


def e4m3fn_values(b):
    return np.asarray(b, np.uint8).view(ml_dtypes.float8_e4m3fn).astype(np.float64)


def setup_inputs():
    d = draw0()
    x0 = np.asarray(d['x']).astype(np.float64)
    s = (np.max(np.abs(x0), axis=(0,), keepdims=True) / 448.0).astype(np.float32)
    out = {}
    for k, v in d.items():
        if k == 'x':
            out['x_bytes'] = e4m3fn_bytes(x0 / s.astype(np.float64))
            out['x_scale'] = s
        else:
            out[k] = v
    return out


def reference(x_bytes, x_scale, keys_words, keys_scales, rel_bias, anchor_gain, values_words, values_scales, gate_words, gate_scales, gate_bias):
    return core(e4m3fn_values(x_bytes) * x_scale.astype(np.float64), keys_words, keys_scales, rel_bias, anchor_gain, values_words, values_scales, gate_words, gate_scales, gate_bias)

@@ -1,0 +1,480 @@
+from contextlib import ExitStack
+
+import concourse.mybir as mybir
+from concourse.masks import make_identity
+
+F32 = mybir.dt.float32
+BF16 = mybir.dt.bfloat16
+I32 = mybir.dt.int32
+U32 = mybir.dt.uint32
+U8 = mybir.dt.uint8
+FP8 = mybir.dt.float8_e4m3fn
+FP8X4 = mybir.dt.float8_e4m3fn_x4
+FP4X4 = mybir.dt.float4_e2m1fn_x4
+ALU = mybir.AluOpType
+ACT = mybir.ActivationFunctionType
+AXIS = mybir.AxisListType
+
+P = 128
+M, N, H, D = 1024, 1536, 2, 512
+C = H * D
+IT = M // P
+NG = N // 512
+FLOPS = 2 * M * N * C * 2 + 2 * M * C * C
+
+NT = H * IT
+LAST = NT - 1
+LAST_PARTS = ((0, 1024), (1024, 1536))
+LAST_OUT = ((0, 256), (256, 512))
+
+
+def tile_relative_bias_anchor_attention_f1_kernel(
+    tc, x_bytes, x_scale, keys_words, keys_scales, rel_bias, anchor_gain, values_words, values_scales, gate_words, gate_scales, gate_bias, out
+):
+    nc = tc.nc
+    with ExitStack() as ctx:
+        keep = ctx.enter_context(tc.tile_pool(name="keep", bufs=1))
+        work = ctx.enter_context(tc.tile_pool(name="work", bufs=2))
+        psum = ctx.enter_context(tc.psum_pool(name="psum", bufs=1))
+        ctx.enter_context(tc.manual_schedule())
+
+        scrap = keep.tile([P, 2], F32, name="scrap")
+        nc.vector.memset(scrap[:, 0:1], 0.0)
+        nc.scalar.activation(out=scrap[:, 1:2], in_=scrap[:, 0:1], func=ACT.Exp)
+        ident = keep.tile([P, P], F32, name="ident")
+        make_identity(nc, ident[:])
+        ident_bf = keep.tile([P, P], BF16, name="ident_bf")
+        make_identity(nc, ident_bf[:])
+
+        x_raw = keep.tile([P, IT, C], U8, name="x_raw", align_bytes=64)
+        xs_b = keep.tile([P, C], F32, name="xs_b")
+        keys_w = keep.tile([P, H, 2 * N], U8, name="keys_w", align_bytes=64)
+        vals_w = keep.tile([P, NG, 2 * C], U8, name="vals_w", align_bytes=64)
+        gate_w = keep.tile([P, H, 2 * C], U8, name="gate_w", align_bytes=64)
+        keys_s = keep.tile([P, H, N], U8, name="keys_s", align_bytes=64)
+        vals_s = keep.tile([P, NG, C], U8, name="vals_s", align_bytes=64)
+        gate_s = keep.tile([P, H, C], U8, name="gate_s", align_bytes=64)
+        gain_b = keep.tile([P, H, N], BF16, name="gain_b")
+        gb_rows = keep.tile([P, P], BF16, name="gb_rows")
+        half_gb = keep.tile([P, C // P], F32, name="half_gb")
+        x_codes = keep.tile([P, H, M], U32, name="x_codes", align_bytes=64)
+        x_planes = keep.tile([P, H, M], U8, name="x_planes", align_bytes=64)
+        th = keep.tile([P, C // P, M], F32, name="th")
+
+        for planes in (keys_s, vals_s, gate_s):
+            nc.vector.memset(planes[:].rearrange("p g n -> p (g n)").bitcast(I32), 0)
+        nc.vector.memset(gb_rows[:], 0.0)
+
+        x_rows = x_bytes.rearrange("(i p) c -> i p c", p=P)
+
+        def load_x(i):
+            nc.sync.dma_start(out=x_raw[:, i, :], in_=x_rows[i])
+
+        def load_scale(g):
+            s = slice(512 * g, 512 * (g + 1))
+            nc.sync.dma_start(out=xs_b[:, s], in_=x_scale.rearrange("o k -> (o k)")[s].partition_broadcast(P))
+
+        def load_words(tile, dram, g):
+            nc.sync.dma_start(out=tile[:, g, :].bitcast(I32), in_=dram[g].bitcast(I32))
+
+        def load_planes(tile, dram):
+            rows = dram.bitcast(I32).rearrange("g r n -> r g n")
+            for q in range(4):
+                nc.sync.dma_start(out=tile[32 * q : 32 * q + 4, :, :].bitcast(I32), in_=rows[4 * q : 4 * q + 4])
+
+        bias = {}
+
+        def load_bias(n):
+            if n >= NT:
+                return
+            t = work.tile([P, N], BF16, name="bias", bufs=4)
+            bias[n] = t
+            i, h = n // H, n % H
+            nc.sync.dma_start(out=t[:], in_=rel_bias[h, i * P : (i + 1) * P, :])
+
+        def load_gain(h):
+            nc.sync.dma_start(out=gain_b[:, h, :], in_=anchor_gain[h].partition_broadcast(P))
+
+        load_x(0)
+        load_scale(0)
+        load_scale(1)
+        load_words(keys_w, keys_words, 0)
+        load_planes(keys_s, keys_scales)
+        load_bias(0)
+        load_x(1)
+        load_words(keys_w, keys_words, 1)
+        load_x(2)
+        load_bias(1)
+        load_gain(0)
+        load_x(3)
+        load_gain(1)
+        load_planes(gate_s, gate_scales)
+        load_words(gate_w, gate_words, 0)
+        load_words(gate_w, gate_words, 1)
+        nc.sync.dma_start(out=gb_rows[0 : C // P, :], in_=gate_bias.rearrange("(a b) -> a b", b=P))
+        load_bias(2)
+        load_planes(vals_s, values_scales)
+        for g in range(NG):
+            load_words(vals_w, values_words, g)
+        load_bias(3)
+        for i in range(4, IT):
+            load_x(i)
+
+        x_bf, x_ps, x_grp = {}, {}, {}
+
+        def x_mult(i, gs=(0, 1)):
+            if i not in x_bf:
+                x_bf[i] = work.tile([P, C], BF16, name="x_bf", bufs=3)
+            s = slice(512 * gs[0], 512 * (gs[-1] + 1))
+            nc.vector.tensor_tensor(out=x_bf[i][:, s], in0=x_raw[:, i, s].bitcast(FP8), in1=xs_b[:, s], op=ALU.mult)
+
+        def x_turn(i, gs=(0, 1)):
+            t = psum.tile([P, 4, P], F32, name="tr", bufs=2)
+            x_ps[i] = t
+            words = x_bf[i][:].bitcast(F32)
+            for k, g in enumerate(gs):
+                for u in range(2):
+                    nc.tensor.transpose(t[:, 2 * k + u, :], words[:, 256 * g + u : 256 * (g + 1) : 2], ident[:])
+
+        def x_copy(i, gs=(0, 1)):
+            n = len(gs)
+            t = work.tile([P, H, P, 4], BF16, name="x_grp", bufs=2, align_bytes=64)
+            x_grp[i] = t
+            nc.scalar.copy(
+                out=t[:, 0:n, :, :].rearrange("p g r t -> p (g r t)").bitcast(F32).rearrange("p (g r u) -> p g r u", g=n, u=2),
+                in_=x_ps[i][:, 0 : 2 * n, :].rearrange("p (g u) r -> p g r u", u=2),
+            )
+
+        def x_quant(i, gs=(0, 1)):
+            for k, g in enumerate(gs):
+                nc.vector.quantize_mx(
+                    out=x_codes[:, g, i * P : (i + 1) * P].bitcast(FP8X4),
+                    scales=x_planes[:, g, i * P : (i + 1) * P],
+                    in_=x_grp[i][:, k, :, :].rearrange("p r t -> p (r t)"),
+                )
+
+        score = {}
+
+        def scores(n):
+            if n >= NT:
+                return
+            i, h = n // H, n % H
+            for j in range(NG):
+                t = psum.tile([P, 512], F32, name="sc", bufs=3)
+                score[n, j] = t
+                nc.tensor.matmul_mx(
+                    out=t[:],
+                    lhsT=x_codes[:, h, i * P : (i + 1) * P].bitcast(FP8X4),
+                    lhsT_scale=x_planes[:, h, i * P : (i + 1) * P],
+                    rhs=keys_w[:, h, 1024 * j : 1024 * (j + 1)].bitcast(FP4X4),
+                    rhs_scale=keys_s[:, h, 512 * j : 512 * (j + 1)],
+                    start=True,
+                    stop=True,
+                )
+
+        neg, nmax, esum, e_t, u_t, u_ps, grp, codes, planes_u, num, numr, rinv, twice_t, sg, raw = ({} for _ in range(15))
+        OFF = ()
+
+        def add_part(n, j):
+            if n in OFF:
+                return
+            if j == 0:
+                neg[n] = work.tile([P, N], F32, name="neg", bufs=3)
+            nc.vector.scalar_tensor_tensor(
+                out=neg[n][:, 512 * j : 512 * (j + 1)],
+                in0=score[n, j][:],
+                scalar=-1.0,
+                in1=bias[n][:, 512 * j : 512 * (j + 1)],
+                op0=ALU.mult,
+                op1=ALU.subtract,
+            )
+
+        def add_a(n):
+            add_part(n, 0)
+
+        def add_b(n):
+            add_part(n, 1)
+
+        def add_c(n):
+            add_part(n, 2)
+
+        def evac(n):
+            if n not in OFF:
+                return
+            raw[n] = work.tile([P, N], F32, name="raw", bufs=1)
+            for j in range(NG):
+                nc.scalar.activation(out=raw[n][:, 512 * j : 512 * (j + 1)], in_=score[n, j][:], func=ACT.Copy, scale=-1.0)
+
+        def off_add(n):
+            if n not in OFF:
+                return
+            neg[n] = work.tile([P, N], F32, name="neg", bufs=3)
+            nc.gpsimd.tensor_tensor(out=neg[n][:], in0=raw[n][:], in1=bias[n][:], op=ALU.subtract)
+
+        def row_max(n):
+            nmax[n] = work.tile([P, 1], F32, name="nmax", bufs=3)
+            nc.vector.tensor_reduce(out=nmax[n][:], in_=neg[n][:], axis=AXIS.X, op=ALU.min)
+
+        def expo(n):
+            e_t[n] = work.tile([P, N], F32, name="e_t", bufs=3)
+            esum[n] = work.tile([P, 2], F32, name="esum", bufs=6)
+            if n == LAST:
+                for k, (a, b) in enumerate(LAST_PARTS):
+                    s = slice(a, b)
+                    nc.scalar.activation(out=e_t[n][:, s], in_=neg[n][:, s], func=ACT.Exp, bias=nmax[n][:], scale=-1.0, accum_out=esum[n][:, k : k + 1])
+                return
+            nc.scalar.activation(out=e_t[n][:], in_=neg[n][:], func=ACT.Exp, bias=nmax[n][:], scale=-1.0, accum_out=esum[n][:, 0:1])
+
+        GP = ((0, 1536),)
+
+        def gains(n):
+            h = n % H
+            u_t[n] = work.tile([P, N], BF16, name="u_t", bufs=5)
+            for a, b in GP:
+                nc.gpsimd.tensor_tensor(out=u_t[n][:, a:b], in0=e_t[n][:, a:b], in1=gain_b[:, h, a:b], op=ALU.mult)
+
+        def last_gains(k):
+            n = LAST
+            a, b = LAST_PARTS[k]
+            if k == 0:
+                u_t[n] = work.tile([P, N], BF16, name="u_t", bufs=5)
+            nc.vector.tensor_tensor(out=u_t[n][:, a:b], in0=e_t[n][:, a:b], in1=gain_b[:, n % H, a:b], op=ALU.mult)
+
+        def turn_part(n, part, gs):
+            words = u_t[n][:].bitcast(F32)
+            t = psum.tile([P, 4, P], F32, name="tr", bufs=2)
+            u_ps[n, part] = t
+            for k, g in enumerate(gs):
+                for u in range(2):
+                    nc.tensor.transpose(t[:, 2 * k + u, :], words[:, 256 * g + u : 256 * (g + 1) : 2], ident[:])
+
+        def turn(n):
+            turn_part(n, 0, (0, 1))
+            turn_part(n, 1, (2,))
+
+        def turn_copy_part(n, part, g0, ng, eng):
+            if part == 0:
+                grp[n] = work.tile([P, NG, P, 4], BF16, name="grp", bufs=3, align_bytes=64)
+            dst = grp[n][:, g0 : g0 + ng, :, :].rearrange("p g r t -> p (g r t)").bitcast(F32)
+            eng(
+                out=dst.rearrange("p (g r u) -> p g r u", g=ng, u=2),
+                in_=u_ps[n, part][:, 0 : 2 * ng, :].rearrange("p (g u) r -> p g r u", u=2),
+            )
+
+        def turn_copy(n):
+            turn_copy_part(n, 0, 0, 2, nc.scalar.copy)
+            turn_copy_part(n, 1, 2, 1, nc.scalar.copy)
+
+        def quant_part(n, g0, ng):
+            if g0 == 0:
+                codes[n] = work.tile([P, NG * P], U32, name="codes", bufs=4, align_bytes=64)
+                planes_u[n] = work.tile([P, NG * P], U8, name="planes_u", bufs=4, align_bytes=64)
+            s = slice(g0 * P, (g0 + ng) * P)
+            nc.vector.quantize_mx(
+                out=codes[n][:, s].bitcast(FP8X4),
+                scales=planes_u[n][:, s],
+                in_=grp[n][:, g0 : g0 + ng, :, :].rearrange("p g r t -> p (g r t)"),
+            )
+
+        def quant(n):
+            quant_part(n, 0, 2)
+            quant_part(n, 2, 1)
+
+        def weigh_part(n, g):
+            h = n % H
+            if g == 0:
+                num[n] = psum.tile([P, 512], F32, name="num", bufs=2)
+            s = slice(g * P, (g + 1) * P)
+            nc.tensor.matmul_mx(
+                out=num[n][:],
+                lhsT=codes[n][:, s].bitcast(FP8X4),
+                lhsT_scale=planes_u[n][:, s],
+                rhs=vals_w[:, g, 1024 * h : 1024 * (h + 1)].bitcast(FP4X4),
+                rhs_scale=vals_s[:, g, 512 * h : 512 * (h + 1)],
+                start=(g == 0),
+                stop=(g == NG - 1),
+            )
+
+        def weigh(n):
+            for g in range(NG):
+                weigh_part(n, g)
+
+        def double(n):
+            twice_t[n] = work.tile([P, 1], F32, name="twice", bufs=6)
+            if n == LAST:
+                nc.vector.tensor_scalar(out=twice_t[n][:], in0=esum[n][:, 0:1], scalar1=esum[n][:, 1:2], scalar2=2.0, op0=ALU.add, op1=ALU.mult)
+                return
+            nc.scalar.activation(out=twice_t[n][:], in_=esum[n][:, 0:1], func=ACT.Copy, scale=2.0)
+
+        def inverse(n):
+            rinv[n] = work.tile([P, 1], F32, name="rinv", bufs=6)
+            nc.vector.reciprocal(out=rinv[n][:], in_=twice_t[n][:])
+
+        def norm(n):
+            numr[n] = work.tile([P, 512], F32, name="numr", bufs=4)
+            if n == LAST:
+                for a, b in LAST_OUT:
+                    nc.scalar.activation(out=numr[n][:, a:b], in_=num[n][:, a:b], func=ACT.Copy, scale=rinv[n][:])
+                return
+            nc.scalar.activation(out=numr[n][:], in_=num[n][:], func=ACT.Copy, scale=rinv[n][:])
+
+        z_ps = {}
+
+        def gate_mm(half, cb):
+            z_ps[half, cb] = psum.tile([P, 512], F32, name="tr", bufs=2)
+            s = slice(512 * half, 512 * (half + 1))
+            for g in range(H):
+                nc.tensor.matmul_mx(
+                    out=z_ps[half, cb][:],
+                    lhsT=gate_w[:, g, 256 * cb : 256 * (cb + 1)].bitcast(FP4X4),
+                    lhsT_scale=gate_s[:, g, P * cb : P * (cb + 1)],
+                    rhs=x_codes[:, g, s].bitcast(FP8X4),
+                    rhs_scale=x_planes[:, g, s],
+                    start=(g == 0),
+                    stop=(g == H - 1),
+                )
+
+        def gate_tanh(half, cb):
+            s = slice(512 * half, 512 * (half + 1))
+            nc.scalar.activation(out=th[:, cb, s], in_=z_ps[half, cb][:], func=ACT.Tanh, bias=half_gb[:, cb : cb + 1], scale=0.5)
+
+        def gate_turn(n):
+            i, h = n // H, n % H
+            if 11 <= n < LAST - 1:
+                sg[n] = psum.tile([P, 4, P], F32, name="sc", bufs=3)
+            elif n == LAST:
+                sg[n] = psum.tile([P, 4, P], F32, name="tr", bufs=2)
+            else:
+                sg[n] = psum.tile([P, 4, P], F32, name="sg", bufs=1)
+            for q in range(4):
+                nc.tensor.transpose(sg[n][:, q, :], th[:, 4 * h + q, i * P : (i + 1) * P], ident[:])
+
+        def final_part(n, a, b):
+            i, h = n // H, n % H
+            o = work.tile([P, b - a], F32, name="o_t", bufs=4)
+            nc.vector.scalar_tensor_tensor(
+                out=o[:],
+                in0=sg[n][:].rearrange("p q r -> p (q r)")[:, a:b],
+                scalar=1.0,
+                in1=numr[n][:, a:b],
+                op0=ALU.add,
+                op1=ALU.mult,
+            )
+            nc.sync.dma_start(out=out[i * P : (i + 1) * P, 512 * h + a : 512 * h + b], in_=o[:])
+
+        def final(n):
+            if n == LAST:
+                for a, b in LAST_OUT:
+                    final_part(n, a, b)
+                return
+            final_part(n, 0, 512)
+
+        def gb_prep():
+            gb_ps = psum.tile([P, P], BF16, name="tr", bufs=2)
+            nc.tensor.transpose(gb_ps[:], gb_rows[:], ident_bf[:])
+            nc.scalar.activation(out=half_gb[:], in_=gb_ps[:, 0 : C // P], func=ACT.Copy, scale=0.5)
+
+        def x_at(fn, name):
+            def go(k):
+                for i in XT[name].get(k, ()):
+                    fn(i)
+
+            return go
+
+        def gates(k):
+            for half, cb in GT.get(k, ()):
+                gate_mm(half, cb)
+                gate_tanh(half, cb)
+
+        def bias_next(n):
+            load_bias(n + 4)
+
+        def score_next(n):
+            scores(n + 1)
+
+        x_mult(0, (0,))
+        x_turn(0, (0,))
+        x_copy(0, (0,))
+        x_mult(0, (1,))
+        x_quant(0, (0,))
+        scores(0)
+        x_turn(0, (1,))
+        x_copy(0, (1,))
+        x_mult(1)
+        x_quant(0, (1,))
+        x_turn(1)
+        x_copy(1)
+
+        XT = {"mult": {0: (2,), 1: (3,), 3: (4,), 4: (5,), 5: (6,), 6: (7,)}, "turn": {0: (2,), 1: (3,), 3: (4,), 4: (5,), 5: (6,), 6: (7,)}, "quant": {0: (1,), 1: (2,), 2: (3,), 4: (4,), 5: (5,), 6: (6,), 7: (7,)}}
+        GT = {3: ((0, 0), (0, 1)), 4: ((0, 2), (0, 3)), 5: ((0, 4), (0, 5)), 6: ((0, 6), (0, 7)), 8: ((1, 0), (1, 1)), 9: ((1, 2), (1, 3)), 10: ((1, 4), (1, 5)), 11: ((1, 6), (1, 7))}
+        seq = (
+            (turn, 3),
+            (turn_copy, 3),
+            (gate_turn, 6),
+            (add_a, 0),
+            (add_b, 0),
+            (quant, 4),
+            (x_at(x_quant, "quant"), None),
+            (x_at(x_mult, "mult"), None),
+            (add_c, 0),
+            (bias_next, 0),
+            (score_next, 0),
+            (weigh, 4),
+            (double, 1),
+            (norm, 5),
+            (x_at(x_turn, "turn"), None),
+            (x_at(x_copy, "turn"), None),
+            (inverse, 2),
+            (final, 6),
+            (row_max, 0),
+            (gates, None),
+            (expo, 0),
+            (gains, 0),
+        )
+        for k in range(NT):
+            if k == 2:
+                gb_prep()
+            for fn, lag in seq:
+                if k == LAST and fn is gates:
+                    break
+                if lag is None:
+                    fn(k)
+                elif 0 <= k - lag < NT:
+                    fn(k - lag)
+        turn(13)
+        turn_copy(13)
+        expo(15)
+        gate_turn(10)
+        gate_turn(11)
+        gate_turn(12)
+        gate_turn(13)
+        quant(12)
+        weigh(12)
+        norm(11)
+        final(10)
+        gate_turn(14)
+        last_gains(0)
+        turn(14)
+        turn_copy(14)
+        final(11)
+        last_gains(1)
+        quant(13)
+        weigh(13)
+        turn(15)
+        norm(12)
+        turn_copy(15)
+        gate_turn(15)
+        final(12)
+        inverse(14)
+        quant(14)
+        weigh(14)
+        norm(13)
+        double(15)
+        quant(15)
+        inverse(15)
+        weigh(15)
+        final(13)
+        norm(14)
+        final(14)
+        norm(15)
+        final(15)

@@ -97,9 +97,9 @@ def tile_relative_bias_anchor_attention_f1_kernel(
 
         load_x(0)
         load_scale(0)
+        load_planes(keys_s, keys_scales)
         load_scale(1)
         load_words(keys_w, keys_words, 0)
-        load_planes(keys_s, keys_scales)
         load_bias(0)
         load_x(1)
         load_words(keys_w, keys_words, 1)
@@ -225,13 +225,32 @@ def tile_relative_bias_anchor_attention_f1_kernel(
                 return
             nc.scalar.activation(out=e_t[n][:], in_=neg[n][:], func=ACT.Exp, bias=nmax[n][:], scale=-1.0, accum_out=esum[n][:, 0:1])
 
-        GP = ((0, 1536),)
+        GP = ((0, 1280),)
 
         def gains(n):
             h = n % H
             u_t[n] = work.tile([P, N], BF16, name="u_t", bufs=5)
             for a, b in GP:
                 nc.gpsimd.tensor_tensor(out=u_t[n][:, a:b], in0=e_t[n][:, a:b], in1=gain_b[:, h, a:b], op=ALU.mult)
+
+        def gains_v(n):
+            if n == LAST:
+                return
+            s = slice(1280, N)
+            nc.vector.tensor_tensor(out=u_t[n][:, s], in0=e_t[n][:, s], in1=gain_b[:, n % H, s], op=ALU.mult)
+
+        def shared_port(early):
+            def go(k):
+                if early != (k < EARLY):
+                    return
+                if 0 <= k - QL < NT:
+                    quant(k - QL)
+                if 0 <= k - 2 < NT:
+                    gains_v(k - 2)
+                x_at(x_quant, "quant")(k)
+                x_at(x_mult, "mult")(k)
+
+            return go
 
         def last_gains(k):
             n = LAST
@@ -405,17 +424,17 @@ def tile_relative_bias_anchor_attention_f1_kernel(
         x_turn(1)
         x_copy(1)
 
+        EARLY = 0
+        QL = 4
         XT = {"mult": {0: (2,), 1: (3,), 3: (4,), 4: (5,), 5: (6,), 6: (7,)}, "turn": {0: (2,), 1: (3,), 3: (4,), 4: (5,), 5: (6,), 6: (7,)}, "quant": {0: (1,), 1: (2,), 2: (3,), 4: (4,), 5: (5,), 6: (6,), 7: (7,)}}
-        GT = {3: ((0, 0), (0, 1)), 4: ((0, 2), (0, 3)), 5: ((0, 4), (0, 5)), 6: ((0, 6), (0, 7)), 8: ((1, 0), (1, 1)), 9: ((1, 2), (1, 3)), 10: ((1, 4), (1, 5)), 11: ((1, 6), (1, 7))}
+        GT = {2: ((0, 0), (0, 1)), 3: ((0, 2), (0, 3)), 4: ((0, 4), (0, 5)), 5: ((0, 6), (0, 7)), 8: ((1, 0), (1, 1)), 9: ((1, 2), (1, 3)), 10: ((1, 4), (1, 5)), 11: ((1, 6), (1, 7))}
         seq = (
             (turn, 3),
             (turn_copy, 3),
-            (gate_turn, 6),
+            (shared_port(True), None),
             (add_a, 0),
             (add_b, 0),
-            (quant, 4),
-            (x_at(x_quant, "quant"), None),
-            (x_at(x_mult, "mult"), None),
+            (shared_port(False), None),
             (add_c, 0),
             (bias_next, 0),
             (score_next, 0),
@@ -427,12 +446,13 @@ def tile_relative_bias_anchor_attention_f1_kernel(
             (inverse, 2),
             (final, 6),
             (row_max, 0),
+            (gate_turn, 5),
             (gates, None),
             (expo, 0),
             (gains, 0),
         )
         for k in range(NT):
-            if k == 2:
+            if k == 1:
                 gb_prep()
             for fn, lag in seq:
                 if k == LAST and fn is gates:
@@ -441,10 +461,10 @@ def tile_relative_bias_anchor_attention_f1_kernel(
                     fn(k)
                 elif 0 <= k - lag < NT:
                     fn(k - lag)
+        gains_v(14)
         turn(13)
         turn_copy(13)
         expo(15)
-        gate_turn(10)
         gate_turn(11)
         gate_turn(12)
         gate_turn(13)

@@ -70,9 +70,11 @@ def tile_relative_bias_anchor_attention_f1_kernel(
         def load_x(i):
             nc.sync.dma_start(out=x_raw[:, i, :], in_=x_rows[i])
 
-        def load_scale(g):
-            s = slice(512 * g, 512 * (g + 1))
-            nc.sync.dma_start(out=xs_b[:, s], in_=x_scale.rearrange("o k -> (o k)")[s].partition_broadcast(P))
+        xs_8 = keep.tile([P, C // P], F32, name="xs_8")
+        ones = keep.tile([P, P], BF16, name="ones")
+        nc.vector.memset(ones[:], 1.0)
+        gain_rows = keep.tile([P, H * N], BF16, name="gain_rows")
+        nc.gpsimd.memset(gain_rows[:].bitcast(I32), 0)
 
         def load_words(tile, dram, g):
             nc.sync.dma_start(out=tile[:, g, :].bitcast(I32), in_=dram[g].bitcast(I32))
@@ -92,27 +94,40 @@ def tile_relative_bias_anchor_attention_f1_kernel(
             i, h = n // H, n % H
             nc.sync.dma_start(out=t[:], in_=rel_bias[h, i * P : (i + 1) * P, :])
 
-        def load_gain(h):
-            nc.sync.dma_start(out=gain_b[:, h, :], in_=anchor_gain[h].partition_broadcast(P))
+        def scale_spread():
+            for b in range(2):
+                t = psum.tile([P, 4, P], F32, name="sg", bufs=2)
+                for k in range(4):
+                    m = 4 * b + k
+                    nc.tensor.transpose(t[:, k, :], xs_8[:, m : m + 1].to_broadcast([P, P]), ident[:])
+                copy = (nc.scalar.copy, nc.vector.tensor_copy)[b]
+                copy(out=xs_b[:].rearrange("q (p b k) -> q b p k", b=2, k=4)[:, b, :, :], in_=t[:].rearrange("q k p -> q p k"))
 
+        def gain_spread(h, gs):
+            for g in gs:
+                t = psum.tile([P, 512], F32, name="sg", bufs=2)
+                nc.tensor.matmul(t[:], lhsT=ones[:], rhs=gain_rows[:, h * N + 512 * g : h * N + 512 * (g + 1)], start=True, stop=True)
+                nc.scalar.copy(
+                    out=gain_b[:, h, 512 * g : 512 * (g + 1)].rearrange("p (u m e) -> p u m e", u=2, e=2),
+                    in_=t[:].rearrange("p (m u e) -> p u m e", u=2, e=2),
+                )
+
+        nc.sync.dma_start(out=xs_8[:], in_=x_scale.rearrange("o (p m) -> p (o m)", p=P))
         load_x(0)
-        load_scale(0)
         load_planes(keys_s, keys_scales)
-        load_scale(1)
         load_words(keys_w, keys_words, 0)
         load_bias(0)
         load_x(1)
+        nc.sync.dma_start(out=gain_rows[0:1, :], in_=anchor_gain.rearrange("(o h) n -> o (h n)", o=1))
         load_words(keys_w, keys_words, 1)
-        load_x(2)
         load_bias(1)
-        load_gain(0)
+        load_x(2)
         load_x(3)
-        load_gain(1)
+        nc.sync.dma_start(out=gb_rows[0 : C // P, :], in_=gate_bias.rearrange("(a b) -> a b", b=P))
         load_planes(gate_s, gate_scales)
+        load_bias(2)
         load_words(gate_w, gate_words, 0)
         load_words(gate_w, gate_words, 1)
-        nc.sync.dma_start(out=gb_rows[0 : C // P, :], in_=gate_bias.rearrange("(a b) -> a b", b=P))
-        load_bias(2)
         load_planes(vals_s, values_scales)
         for g in range(NG):
             load_words(vals_w, values_words, g)
@@ -180,13 +195,11 @@ def tile_relative_bias_anchor_attention_f1_kernel(
                 return
             if j == 0:
                 neg[n] = work.tile([P, N], F32, name="neg", bufs=3)
-            nc.vector.scalar_tensor_tensor(
-                out=neg[n][:, 512 * j : 512 * (j + 1)],
-                in0=score[n, j][:],
-                scalar=-1.0,
-                in1=bias[n][:, 512 * j : 512 * (j + 1)],
-                op0=ALU.mult,
-                op1=ALU.subtract,
+            nc.vector.tensor_tensor(
+                out=neg[n][:, 512 * j : 512 * (j + 1)].rearrange("p (u m e) -> p u m e", u=2, e=2),
+                in0=score[n, j][:].rearrange("p (m u e) -> p u m e", u=2, e=2),
+                in1=bias[n][:, 512 * j : 512 * (j + 1)].rearrange("p (m u e) -> p u m e", u=2, e=2),
+                op=ALU.add,
             )
 
         def add_a(n):
@@ -213,7 +226,7 @@ def tile_relative_bias_anchor_attention_f1_kernel(
 
         def row_max(n):
             nmax[n] = work.tile([P, 1], F32, name="nmax", bufs=3)
-            nc.vector.tensor_reduce(out=nmax[n][:], in_=neg[n][:], axis=AXIS.X, op=ALU.min)
+            nc.vector.tensor_reduce(out=nmax[n][:], in_=neg[n][:], axis=AXIS.X, op=ALU.max, negate=True)
 
         def expo(n):
             e_t[n] = work.tile([P, N], F32, name="e_t", bufs=3)
@@ -221,11 +234,11 @@ def tile_relative_bias_anchor_attention_f1_kernel(
             if n == LAST:
                 for k, (a, b) in enumerate(LAST_PARTS):
                     s = slice(a, b)
-                    nc.scalar.activation(out=e_t[n][:, s], in_=neg[n][:, s], func=ACT.Exp, bias=nmax[n][:], scale=-1.0, accum_out=esum[n][:, k : k + 1])
+                    nc.scalar.activation(out=e_t[n][:, s], in_=neg[n][:, s], func=ACT.Exp, bias=nmax[n][:], scale=1.0, accum_out=esum[n][:, k : k + 1])
                 return
-            nc.scalar.activation(out=e_t[n][:], in_=neg[n][:], func=ACT.Exp, bias=nmax[n][:], scale=-1.0, accum_out=esum[n][:, 0:1])
+            nc.scalar.activation(out=e_t[n][:], in_=neg[n][:], func=ACT.Exp, bias=nmax[n][:], scale=1.0, accum_out=esum[n][:, 0:1])
 
-        GP = ((0, 1280),)
+        GP = ((0, 1408),)
 
         def gains(n):
             h = n % H
@@ -236,7 +249,7 @@ def tile_relative_bias_anchor_attention_f1_kernel(
         def gains_v(n):
             if n == LAST:
                 return
-            s = slice(1280, N)
+            s = slice(1408, N)
             nc.vector.tensor_tensor(out=u_t[n][:, s], in0=e_t[n][:, s], in1=gain_b[:, n % H, s], op=ALU.mult)
 
         def shared_port(early):
@@ -265,7 +278,7 @@ def tile_relative_bias_anchor_attention_f1_kernel(
             u_ps[n, part] = t
             for k, g in enumerate(gs):
                 for u in range(2):
-                    nc.tensor.transpose(t[:, 2 * k + u, :], words[:, 256 * g + u : 256 * (g + 1) : 2], ident[:])
+                    nc.tensor.transpose(t[:, 2 * k + u, :], words[:, 256 * g + P * u : 256 * g + P * (u + 1)], ident[:])
 
         def turn(n):
             turn_part(n, 0, (0, 1))
@@ -302,7 +315,10 @@ def tile_relative_bias_anchor_attention_f1_kernel(
         def weigh_part(n, g):
             h = n % H
             if g == 0:
-                num[n] = psum.tile([P, 512], F32, name="num", bufs=2)
+                if n > NT - 4:
+                    num[n] = psum.tile([P, 512], F32, name="sc", bufs=3)
+                else:
+                    num[n] = psum.tile([P, 512], F32, name="num", bufs=1)
             s = slice(g * P, (g + 1) * P)
             nc.tensor.matmul_mx(
                 out=num[n][:],
@@ -359,12 +375,10 @@ def tile_relative_bias_anchor_attention_f1_kernel(
 
         def gate_turn(n):
             i, h = n // H, n % H
-            if 11 <= n < LAST - 1:
-                sg[n] = psum.tile([P, 4, P], F32, name="sc", bufs=3)
-            elif n == LAST:
+            if n == LAST:
                 sg[n] = psum.tile([P, 4, P], F32, name="tr", bufs=2)
             else:
-                sg[n] = psum.tile([P, 4, P], F32, name="sg", bufs=1)
+                sg[n] = psum.tile([P, 4, P], F32, name="sg", bufs=2)
             for q in range(4):
                 nc.tensor.transpose(sg[n][:, q, :], th[:, 4 * h + q, i * P : (i + 1) * P], ident[:])
 
@@ -411,42 +425,44 @@ def tile_relative_bias_anchor_attention_f1_kernel(
         def score_next(n):
             scores(n + 1)
 
+        scale_spread()
         x_mult(0, (0,))
         x_turn(0, (0,))
         x_copy(0, (0,))
         x_mult(0, (1,))
+        x_turn(0, (1,))
         x_quant(0, (0,))
         scores(0)
-        x_turn(0, (1,))
         x_copy(0, (1,))
         x_mult(1)
         x_quant(0, (1,))
         x_turn(1)
         x_copy(1)
+        gain_spread(0, (0, 1, 2))
+        gain_spread(1, (0, 1, 2))
 
         EARLY = 0
         QL = 4
         XT = {"mult": {0: (2,), 1: (3,), 3: (4,), 4: (5,), 5: (6,), 6: (7,)}, "turn": {0: (2,), 1: (3,), 3: (4,), 4: (5,), 5: (6,), 6: (7,)}, "quant": {0: (1,), 1: (2,), 2: (3,), 4: (4,), 5: (5,), 6: (6,), 7: (7,)}}
         GT = {2: ((0, 0), (0, 1)), 3: ((0, 2), (0, 3)), 4: ((0, 4), (0, 5)), 5: ((0, 6), (0, 7)), 8: ((1, 0), (1, 1)), 9: ((1, 2), (1, 3)), 10: ((1, 4), (1, 5)), 11: ((1, 6), (1, 7))}
         seq = (
+            (weigh, 5),
+            (norm, 5),
             (turn, 3),
             (turn_copy, 3),
-            (shared_port(True), None),
+            (gate_turn, 5),
             (add_a, 0),
             (add_b, 0),
             (shared_port(False), None),
             (add_c, 0),
             (bias_next, 0),
             (score_next, 0),
-            (weigh, 4),
             (double, 1),
-            (norm, 5),
             (x_at(x_turn, "turn"), None),
             (x_at(x_copy, "turn"), None),
             (inverse, 2),
             (final, 6),
             (row_max, 0),
-            (gate_turn, 5),
             (gates, None),
             (expo, 0),
             (gains, 0),
@@ -465,26 +481,27 @@ def tile_relative_bias_anchor_attention_f1_kernel(
         turn(13)
         turn_copy(13)
         expo(15)
+        weigh(11)
         gate_turn(11)
-        gate_turn(12)
-        gate_turn(13)
-        quant(12)
-        weigh(12)
         norm(11)
+        quant(12)
         final(10)
-        gate_turn(14)
+        gate_turn(12)
         last_gains(0)
         turn(14)
+        weigh(12)
         turn_copy(14)
+        norm(12)
         final(11)
         last_gains(1)
+        gate_turn(13)
         quant(13)
-        weigh(13)
         turn(15)
-        norm(12)
         turn_copy(15)
+        weigh(13)
         gate_turn(15)
         final(12)
+        gate_turn(14)
         inverse(14)
         quant(14)
         weigh(14)
@@ -492,9 +509,9 @@ def tile_relative_bias_anchor_attention_f1_kernel(
         double(15)
         quant(15)
         inverse(15)
+        norm(14)
         weigh(15)
         final(13)
-        norm(14)
         final(14)
         norm(15)
         final(15)

@@ -24,6 +24,7 @@ FLOPS = 2 * M * N * C * 2 + 2 * M * C * C
 
 NT = H * IT
 LAST = NT - 1
+CUT = 1536
 LAST_PARTS = ((0, 1024), (1024, 1536))
 LAST_OUT = ((0, 256), (256, 512))
 
@@ -44,10 +45,9 @@ def tile_relative_bias_anchor_attention_f1_kernel(
         ident = keep.tile([P, P], F32, name="ident")
         make_identity(nc, ident[:])
         ident_bf = keep.tile([P, P], BF16, name="ident_bf")
-        make_identity(nc, ident_bf[:])
 
         x_raw = keep.tile([P, IT, C], U8, name="x_raw", align_bytes=64)
-        xs_b = keep.tile([P, C], F32, name="xs_b")
+        xs4 = keep.tile([P, H, 4], F32, name="xs4")
         keys_w = keep.tile([P, H, 2 * N], U8, name="keys_w", align_bytes=64)
         vals_w = keep.tile([P, NG, 2 * C], U8, name="vals_w", align_bytes=64)
         gate_w = keep.tile([P, H, 2 * C], U8, name="gate_w", align_bytes=64)
@@ -55,26 +55,24 @@ def tile_relative_bias_anchor_attention_f1_kernel(
         vals_s = keep.tile([P, NG, C], U8, name="vals_s", align_bytes=64)
         gate_s = keep.tile([P, H, C], U8, name="gate_s", align_bytes=64)
         gain_b = keep.tile([P, H, N], BF16, name="gain_b")
+        gain_rows = keep.tile([P, H * N], BF16, name="gain_rows")
         gb_rows = keep.tile([P, P], BF16, name="gb_rows")
         half_gb = keep.tile([P, C // P], F32, name="half_gb")
+        ones = keep.tile([P, P], BF16, name="ones")
         x_codes = keep.tile([P, H, M], U32, name="x_codes", align_bytes=64)
         x_planes = keep.tile([P, H, M], U8, name="x_planes", align_bytes=64)
         th = keep.tile([P, C // P, M], F32, name="th")
 
+        nc.gpsimd.memset(gain_rows[:].bitcast(I32), 0)
         for planes in (keys_s, vals_s, gate_s):
             nc.vector.memset(planes[:].rearrange("p g n -> p (g n)").bitcast(I32), 0)
         nc.vector.memset(gb_rows[:], 0.0)
+        nc.vector.memset(ones[:], 1.0)
 
         x_rows = x_bytes.rearrange("(i p) c -> i p c", p=P)
 
         def load_x(i):
             nc.sync.dma_start(out=x_raw[:, i, :], in_=x_rows[i])
-
-        xs_8 = keep.tile([P, C // P], F32, name="xs_8")
-        ones = keep.tile([P, P], BF16, name="ones")
-        nc.vector.memset(ones[:], 1.0)
-        gain_rows = keep.tile([P, H * N], BF16, name="gain_rows")
-        nc.gpsimd.memset(gain_rows[:].bitcast(I32), 0)
 
         def load_words(tile, dram, g):
             nc.sync.dma_start(out=tile[:, g, :].bitcast(I32), in_=dram[g].bitcast(I32))
@@ -94,14 +92,66 @@ def tile_relative_bias_anchor_attention_f1_kernel(
             i, h = n // H, n % H
             nc.sync.dma_start(out=t[:], in_=rel_bias[h, i * P : (i + 1) * P, :])
 
-        def scale_spread():
-            for b in range(2):
-                t = psum.tile([P, 4, P], F32, name="sg", bufs=2)
-                for k in range(4):
-                    m = 4 * b + k
-                    nc.tensor.transpose(t[:, k, :], xs_8[:, m : m + 1].to_broadcast([P, P]), ident[:])
-                copy = (nc.scalar.copy, nc.vector.tensor_copy)[b]
-                copy(out=xs_b[:].rearrange("q (p b k) -> q b p k", b=2, k=4)[:, b, :, :], in_=t[:].rearrange("q k p -> q p k"))
+        nc.gpsimd.dma_start(out=gain_rows[0:1, :], in_=anchor_gain.rearrange("(o h) n -> o (h n)", o=1))
+        nc.gpsimd.dma_start(out=gb_rows[0 : C // P, :], in_=gate_bias.rearrange("(a b) -> a b", b=P))
+        load_x(0)
+        nc.sync.dma_start(out=xs4[:], in_=x_scale.rearrange("o (g p t) -> p (o g) t", p=P, t=4))
+        load_x(1)
+        load_planes(keys_s, keys_scales)
+        load_words(keys_w, keys_words, 0)
+        load_bias(0)
+        load_x(2)
+        load_words(keys_w, keys_words, 1)
+        load_bias(1)
+        load_x(3)
+        load_bias(2)
+        load_x(4)
+        load_planes(vals_s, values_scales)
+        for g in range(NG):
+            load_words(vals_w, values_words, g)
+        load_planes(gate_s, gate_scales)
+        load_words(gate_w, gate_words, 0)
+        load_words(gate_w, gate_words, 1)
+        load_bias(3)
+        for i in range(5, IT):
+            load_x(i)
+
+        make_identity(nc, ident_bf[:])
+
+        x_bf, x_ps, x_grp = {}, {}, {}
+
+        def x_cast(i, gs=(0, 1), copy=nc.scalar.copy):
+            if i not in x_bf:
+                x_bf[i] = work.tile([P, C], BF16, name="x_bf", bufs=4)
+            s = slice(512 * gs[0], 512 * (gs[-1] + 1))
+            copy(out=x_bf[i][:, s], in_=x_raw[:, i, s].bitcast(FP8))
+
+        def x_turn(i, gs=(0, 1)):
+            words = x_bf[i][:].bitcast(F32)
+            t = psum.tile([P, 4, P], F32, name="tr", bufs=2)
+            for k, g in enumerate(gs):
+                x_ps[i, g] = t[:, 2 * k : 2 * k + 2, :]
+                for u in range(2):
+                    nc.tensor.transpose(t[:, 2 * k + u, :], words[:, 256 * g + u : 256 * (g + 1) : 2], ident[:])
+
+        def x_mult(i, gs=(0, 1)):
+            if i not in x_grp:
+                x_grp[i] = work.tile([P, H, P, 4], BF16, name="x_grp", bufs=3, align_bytes=64)
+            for g in gs:
+                nc.vector.tensor_tensor(
+                    out=x_grp[i][:, g, :, :].rearrange("p r (u e) -> p r u e", e=2),
+                    in0=x_ps[i, g].bitcast(BF16).rearrange("p u (r e) -> p r u e", e=2),
+                    in1=xs4[:, g, :].unsqueeze(1).to_broadcast([P, P, 4]).rearrange("p r (u e) -> p r u e", e=2),
+                    op=ALU.mult,
+                )
+
+        def x_quant(i, gs=(0, 1)):
+            for g in gs:
+                nc.vector.quantize_mx(
+                    out=x_codes[:, g, i * P : (i + 1) * P].bitcast(FP8X4),
+                    scales=x_planes[:, g, i * P : (i + 1) * P],
+                    in_=x_grp[i][:, g, :, :].rearrange("p r t -> p (r t)"),
+                )
 
         def gain_spread(h, gs):
             for g in gs:
@@ -110,62 +160,6 @@ def tile_relative_bias_anchor_attention_f1_kernel(
                 nc.scalar.copy(
                     out=gain_b[:, h, 512 * g : 512 * (g + 1)].rearrange("p (u m e) -> p u m e", u=2, e=2),
                     in_=t[:].rearrange("p (m u e) -> p u m e", u=2, e=2),
-                )
-
-        nc.sync.dma_start(out=xs_8[:], in_=x_scale.rearrange("o (p m) -> p (o m)", p=P))
-        load_x(0)
-        load_planes(keys_s, keys_scales)
-        load_words(keys_w, keys_words, 0)
-        load_bias(0)
-        load_x(1)
-        nc.sync.dma_start(out=gain_rows[0:1, :], in_=anchor_gain.rearrange("(o h) n -> o (h n)", o=1))
-        load_words(keys_w, keys_words, 1)
-        load_bias(1)
-        load_x(2)
-        load_x(3)
-        nc.sync.dma_start(out=gb_rows[0 : C // P, :], in_=gate_bias.rearrange("(a b) -> a b", b=P))
-        load_planes(gate_s, gate_scales)
-        load_bias(2)
-        load_words(gate_w, gate_words, 0)
-        load_words(gate_w, gate_words, 1)
-        load_planes(vals_s, values_scales)
-        for g in range(NG):
-            load_words(vals_w, values_words, g)
-        load_bias(3)
-        for i in range(4, IT):
-            load_x(i)
-
-        x_bf, x_ps, x_grp = {}, {}, {}
-
-        def x_mult(i, gs=(0, 1)):
-            if i not in x_bf:
-                x_bf[i] = work.tile([P, C], BF16, name="x_bf", bufs=3)
-            s = slice(512 * gs[0], 512 * (gs[-1] + 1))
-            nc.vector.tensor_tensor(out=x_bf[i][:, s], in0=x_raw[:, i, s].bitcast(FP8), in1=xs_b[:, s], op=ALU.mult)
-
-        def x_turn(i, gs=(0, 1)):
-            t = psum.tile([P, 4, P], F32, name="tr", bufs=2)
-            x_ps[i] = t
-            words = x_bf[i][:].bitcast(F32)
-            for k, g in enumerate(gs):
-                for u in range(2):
-                    nc.tensor.transpose(t[:, 2 * k + u, :], words[:, 256 * g + u : 256 * (g + 1) : 2], ident[:])
-
-        def x_copy(i, gs=(0, 1)):
-            n = len(gs)
-            t = work.tile([P, H, P, 4], BF16, name="x_grp", bufs=2, align_bytes=64)
-            x_grp[i] = t
-            nc.scalar.copy(
-                out=t[:, 0:n, :, :].rearrange("p g r t -> p (g r t)").bitcast(F32).rearrange("p (g r u) -> p g r u", g=n, u=2),
-                in_=x_ps[i][:, 0 : 2 * n, :].rearrange("p (g u) r -> p g r u", u=2),
-            )
-
-        def x_quant(i, gs=(0, 1)):
-            for k, g in enumerate(gs):
-                nc.vector.quantize_mx(
-                    out=x_codes[:, g, i * P : (i + 1) * P].bitcast(FP8X4),
-                    scales=x_planes[:, g, i * P : (i + 1) * P],
-                    in_=x_grp[i][:, k, :, :].rearrange("p r t -> p (r t)"),
                 )
 
         score = {}
@@ -187,180 +181,107 @@ def tile_relative_bias_anchor_attention_f1_kernel(
                     stop=True,
                 )
 
-        neg, nmax, esum, e_t, u_t, u_ps, grp, codes, planes_u, num, numr, rinv, twice_t, sg, raw = ({} for _ in range(15))
-        OFF = ()
+        neg, nmax, esum, e_t, u_t, u_ps, grp, codes, planes_u, num, numr, rinv, twice, sg = ({} for _ in range(14))
 
-        def add_part(n, j):
-            if n in OFF:
-                return
-            if j == 0:
+        def add(n, js):
+            if n not in neg:
                 neg[n] = work.tile([P, N], F32, name="neg", bufs=3)
-            nc.vector.tensor_tensor(
-                out=neg[n][:, 512 * j : 512 * (j + 1)].rearrange("p (u m e) -> p u m e", u=2, e=2),
-                in0=score[n, j][:].rearrange("p (m u e) -> p u m e", u=2, e=2),
-                in1=bias[n][:, 512 * j : 512 * (j + 1)].rearrange("p (m u e) -> p u m e", u=2, e=2),
-                op=ALU.add,
-            )
-
-        def add_a(n):
-            add_part(n, 0)
-
-        def add_b(n):
-            add_part(n, 1)
-
-        def add_c(n):
-            add_part(n, 2)
-
-        def evac(n):
-            if n not in OFF:
-                return
-            raw[n] = work.tile([P, N], F32, name="raw", bufs=1)
-            for j in range(NG):
-                nc.scalar.activation(out=raw[n][:, 512 * j : 512 * (j + 1)], in_=score[n, j][:], func=ACT.Copy, scale=-1.0)
-
-        def off_add(n):
-            if n not in OFF:
-                return
-            neg[n] = work.tile([P, N], F32, name="neg", bufs=3)
-            nc.gpsimd.tensor_tensor(out=neg[n][:], in0=raw[n][:], in1=bias[n][:], op=ALU.subtract)
+            for j in js:
+                s = slice(512 * j, 512 * (j + 1))
+                nc.vector.tensor_tensor(
+                    out=neg[n][:, s].rearrange("p (u m e) -> p u m e", u=2, e=2),
+                    in0=score[n, j][:].rearrange("p (m u e) -> p u m e", u=2, e=2),
+                    in1=bias[n][:, s].rearrange("p (m u e) -> p u m e", u=2, e=2),
+                    op=ALU.add,
+                )
 
         def row_max(n):
             nmax[n] = work.tile([P, 1], F32, name="nmax", bufs=3)
             nc.vector.tensor_reduce(out=nmax[n][:], in_=neg[n][:], axis=AXIS.X, op=ALU.max, negate=True)
 
         def expo(n):
+            i, h = n // H, n % H
             e_t[n] = work.tile([P, N], F32, name="e_t", bufs=3)
-            esum[n] = work.tile([P, 2], F32, name="esum", bufs=6)
-            if n == LAST:
-                for k, (a, b) in enumerate(LAST_PARTS):
-                    s = slice(a, b)
-                    nc.scalar.activation(out=e_t[n][:, s], in_=neg[n][:, s], func=ACT.Exp, bias=nmax[n][:], scale=1.0, accum_out=esum[n][:, k : k + 1])
-                return
-            nc.scalar.activation(out=e_t[n][:], in_=neg[n][:], func=ACT.Exp, bias=nmax[n][:], scale=1.0, accum_out=esum[n][:, 0:1])
+            if h == 0:
+                esum[i] = work.tile([P, H + 1], F32, name="esum", bufs=4)
+            for k, (a, b) in enumerate(LAST_PARTS if n == LAST else ((0, N),)):
+                s = slice(a, b)
+                nc.scalar.activation(out=e_t[n][:, s], in_=neg[n][:, s], func=ACT.Exp, bias=nmax[n][:], scale=1.0, accum_out=esum[i][:, h + k : h + k + 1])
 
-        GP = ((0, 1408),)
-
-        def gains(n):
-            h = n % H
-            u_t[n] = work.tile([P, N], BF16, name="u_t", bufs=5)
-            for a, b in GP:
-                nc.gpsimd.tensor_tensor(out=u_t[n][:, a:b], in0=e_t[n][:, a:b], in1=gain_b[:, h, a:b], op=ALU.mult)
-
-        def gains_v(n):
-            if n == LAST:
-                return
-            s = slice(1408, N)
-            nc.vector.tensor_tensor(out=u_t[n][:, s], in0=e_t[n][:, s], in1=gain_b[:, n % H, s], op=ALU.mult)
-
-        def shared_port(early):
-            def go(k):
-                if early != (k < EARLY):
-                    return
-                if 0 <= k - QL < NT:
-                    quant(k - QL)
-                if 0 <= k - 2 < NT:
-                    gains_v(k - 2)
-                x_at(x_quant, "quant")(k)
-                x_at(x_mult, "mult")(k)
-
-            return go
-
-        def last_gains(k):
-            n = LAST
-            a, b = LAST_PARTS[k]
-            if k == 0:
+        def gains(n, a, b, eng):
+            if n not in u_t:
                 u_t[n] = work.tile([P, N], BF16, name="u_t", bufs=5)
-            nc.vector.tensor_tensor(out=u_t[n][:, a:b], in0=e_t[n][:, a:b], in1=gain_b[:, n % H, a:b], op=ALU.mult)
-
-        def turn_part(n, part, gs):
-            words = u_t[n][:].bitcast(F32)
-            t = psum.tile([P, 4, P], F32, name="tr", bufs=2)
-            u_ps[n, part] = t
-            for k, g in enumerate(gs):
-                for u in range(2):
-                    nc.tensor.transpose(t[:, 2 * k + u, :], words[:, 256 * g + P * u : 256 * g + P * (u + 1)], ident[:])
+            eng.tensor_tensor(out=u_t[n][:, a:b], in0=e_t[n][:, a:b], in1=gain_b[:, n % H, a:b], op=ALU.mult)
 
         def turn(n):
-            turn_part(n, 0, (0, 1))
-            turn_part(n, 1, (2,))
-
-        def turn_copy_part(n, part, g0, ng, eng):
-            if part == 0:
-                grp[n] = work.tile([P, NG, P, 4], BF16, name="grp", bufs=3, align_bytes=64)
-            dst = grp[n][:, g0 : g0 + ng, :, :].rearrange("p g r t -> p (g r t)").bitcast(F32)
-            eng(
-                out=dst.rearrange("p (g r u) -> p g r u", g=ng, u=2),
-                in_=u_ps[n, part][:, 0 : 2 * ng, :].rearrange("p (g u) r -> p g r u", u=2),
-            )
+            words = u_t[n][:].bitcast(F32)
+            for part, gs in enumerate(((0, 1), (2,))):
+                t = psum.tile([P, 4, P], F32, name="tr", bufs=2)
+                u_ps[n, part] = t
+                for k, g in enumerate(gs):
+                    for u in range(2):
+                        nc.tensor.transpose(t[:, 2 * k + u, :], words[:, 256 * g + P * u : 256 * g + P * (u + 1)], ident[:])
 
         def turn_copy(n):
-            turn_copy_part(n, 0, 0, 2, nc.scalar.copy)
-            turn_copy_part(n, 1, 2, 1, nc.scalar.copy)
-
-        def quant_part(n, g0, ng):
-            if g0 == 0:
-                codes[n] = work.tile([P, NG * P], U32, name="codes", bufs=4, align_bytes=64)
-                planes_u[n] = work.tile([P, NG * P], U8, name="planes_u", bufs=4, align_bytes=64)
-            s = slice(g0 * P, (g0 + ng) * P)
-            nc.vector.quantize_mx(
-                out=codes[n][:, s].bitcast(FP8X4),
-                scales=planes_u[n][:, s],
-                in_=grp[n][:, g0 : g0 + ng, :, :].rearrange("p g r t -> p (g r t)"),
-            )
+            grp[n] = work.tile([P, NG, P, 4], BF16, name="grp", bufs=3, align_bytes=64)
+            for part, g0, ng in ((0, 0, 2), (1, 2, 1)):
+                dst = grp[n][:, g0 : g0 + ng, :, :].rearrange("p g r t -> p (g r t)").bitcast(F32)
+                nc.scalar.copy(
+                    out=dst.rearrange("p (g r u) -> p g r u", g=ng, u=2),
+                    in_=u_ps[n, part][:, 0 : 2 * ng, :].rearrange("p (g u) r -> p g r u", u=2),
+                )
 
         def quant(n):
-            quant_part(n, 0, 2)
-            quant_part(n, 2, 1)
-
-        def weigh_part(n, g):
-            h = n % H
-            if g == 0:
-                if n > NT - 4:
-                    num[n] = psum.tile([P, 512], F32, name="sc", bufs=3)
-                else:
-                    num[n] = psum.tile([P, 512], F32, name="num", bufs=1)
-            s = slice(g * P, (g + 1) * P)
-            nc.tensor.matmul_mx(
-                out=num[n][:],
-                lhsT=codes[n][:, s].bitcast(FP8X4),
-                lhsT_scale=planes_u[n][:, s],
-                rhs=vals_w[:, g, 1024 * h : 1024 * (h + 1)].bitcast(FP4X4),
-                rhs_scale=vals_s[:, g, 512 * h : 512 * (h + 1)],
-                start=(g == 0),
-                stop=(g == NG - 1),
-            )
+            codes[n] = work.tile([P, NG * P], U32, name="codes", bufs=4, align_bytes=64)
+            planes_u[n] = work.tile([P, NG * P], U8, name="planes_u", bufs=4, align_bytes=64)
+            for g0, ng in ((0, 2), (2, 1)):
+                s = slice(g0 * P, (g0 + ng) * P)
+                nc.vector.quantize_mx(
+                    out=codes[n][:, s].bitcast(FP8X4),
+                    scales=planes_u[n][:, s],
+                    in_=grp[n][:, g0 : g0 + ng, :, :].rearrange("p g r t -> p (g r t)"),
+                )
 
         def weigh(n):
+            h = n % H
+            if n > NT - 4:
+                num[n] = psum.tile([P, 512], F32, name="sc", bufs=3)
+            else:
+                num[n] = psum.tile([P, 512], F32, name="num", bufs=1)
             for g in range(NG):
-                weigh_part(n, g)
+                s = slice(g * P, (g + 1) * P)
+                nc.tensor.matmul_mx(
+                    out=num[n][:],
+                    lhsT=codes[n][:, s].bitcast(FP8X4),
+                    lhsT_scale=planes_u[n][:, s],
+                    rhs=vals_w[:, g, 1024 * h : 1024 * (h + 1)].bitcast(FP4X4),
+                    rhs_scale=vals_s[:, g, 512 * h : 512 * (h + 1)],
+                    start=(g == 0),
+                    stop=(g == NG - 1),
+                )
 
-        def double(n):
-            twice_t[n] = work.tile([P, 1], F32, name="twice", bufs=6)
-            if n == LAST:
-                nc.vector.tensor_scalar(out=twice_t[n][:], in0=esum[n][:, 0:1], scalar1=esum[n][:, 1:2], scalar2=2.0, op0=ALU.add, op1=ALU.mult)
-                return
-            nc.scalar.activation(out=twice_t[n][:], in_=esum[n][:, 0:1], func=ACT.Copy, scale=2.0)
+        def double(i):
+            if i == IT - 1:
+                nc.vector.tensor_tensor(out=esum[i][:, 1:2], in0=esum[i][:, 1:2], in1=esum[i][:, 2:3], op=ALU.add)
+            twice[i] = work.tile([P, H], F32, name="twice", bufs=5)
+            nc.scalar.activation(out=twice[i][:], in_=esum[i][:, 0:H], func=ACT.Copy, scale=2.0)
 
-        def inverse(n):
-            rinv[n] = work.tile([P, 1], F32, name="rinv", bufs=6)
-            nc.vector.reciprocal(out=rinv[n][:], in_=twice_t[n][:])
+        def inverse(i):
+            rinv[i] = work.tile([P, H], F32, name="rinv", bufs=7)
+            nc.vector.reciprocal(out=rinv[i][:], in_=twice[i][:])
 
         def norm(n):
-            numr[n] = work.tile([P, 512], F32, name="numr", bufs=4)
-            if n == LAST:
-                for a, b in LAST_OUT:
-                    nc.scalar.activation(out=numr[n][:, a:b], in_=num[n][:, a:b], func=ACT.Copy, scale=rinv[n][:])
-                return
-            nc.scalar.activation(out=numr[n][:], in_=num[n][:], func=ACT.Copy, scale=rinv[n][:])
+            i, h = n // H, n % H
+            numr[n] = work.tile([P, 512], F32, name="numr", bufs=8)
+            for a, b in LAST_OUT if n == LAST else ((0, 512),):
+                nc.scalar.activation(out=numr[n][:, a:b], in_=num[n][:, a:b], func=ACT.Copy, scale=rinv[i][:, h : h + 1])
 
-        z_ps = {}
-
-        def gate_mm(half, cb):
-            z_ps[half, cb] = psum.tile([P, 512], F32, name="tr", bufs=2)
+        def gate(half, cb):
+            z = psum.tile([P, 512], F32, name="tr", bufs=2)
             s = slice(512 * half, 512 * (half + 1))
             for g in range(H):
                 nc.tensor.matmul_mx(
-                    out=z_ps[half, cb][:],
+                    out=z[:],
                     lhsT=gate_w[:, g, 256 * cb : 256 * (cb + 1)].bitcast(FP4X4),
                     lhsT_scale=gate_s[:, g, P * cb : P * (cb + 1)],
                     rhs=x_codes[:, g, s].bitcast(FP8X4),
@@ -368,10 +289,7 @@ def tile_relative_bias_anchor_attention_f1_kernel(
                     start=(g == 0),
                     stop=(g == H - 1),
                 )
-
-        def gate_tanh(half, cb):
-            s = slice(512 * half, 512 * (half + 1))
-            nc.scalar.activation(out=th[:, cb, s], in_=z_ps[half, cb][:], func=ACT.Tanh, bias=half_gb[:, cb : cb + 1], scale=0.5)
+            nc.scalar.activation(out=th[:, cb, s], in_=z[:], func=ACT.Tanh, bias=half_gb[:, cb : cb + 1], scale=0.5)
 
         def gate_turn(n):
             i, h = n // H, n % H
@@ -382,136 +300,119 @@ def tile_relative_bias_anchor_attention_f1_kernel(
             for q in range(4):
                 nc.tensor.transpose(sg[n][:, q, :], th[:, 4 * h + q, i * P : (i + 1) * P], ident[:])
 
-        def final_part(n, a, b):
-            i, h = n // H, n % H
-            o = work.tile([P, b - a], F32, name="o_t", bufs=4)
-            nc.vector.scalar_tensor_tensor(
-                out=o[:],
-                in0=sg[n][:].rearrange("p q r -> p (q r)")[:, a:b],
-                scalar=1.0,
-                in1=numr[n][:, a:b],
-                op0=ALU.add,
-                op1=ALU.mult,
-            )
-            nc.sync.dma_start(out=out[i * P : (i + 1) * P, 512 * h + a : 512 * h + b], in_=o[:])
-
         def final(n):
-            if n == LAST:
-                for a, b in LAST_OUT:
-                    final_part(n, a, b)
-                return
-            final_part(n, 0, 512)
+            i, h = n // H, n % H
+            for a, b in LAST_OUT if n == LAST else ((0, 512),):
+                o = work.tile([P, b - a], F32, name="o_t", bufs=4)
+                nc.vector.scalar_tensor_tensor(
+                    out=o[:],
+                    in0=sg[n][:].rearrange("p q r -> p (q r)")[:, a:b],
+                    scalar=1.0,
+                    in1=numr[n][:, a:b],
+                    op0=ALU.add,
+                    op1=ALU.mult,
+                )
+                nc.sync.dma_start(out=out[i * P : (i + 1) * P, 512 * h + a : 512 * h + b], in_=o[:])
 
         def gb_prep():
-            gb_ps = psum.tile([P, P], BF16, name="tr", bufs=2)
+            gb_ps = psum.tile([P, P], BF16, name="sg", bufs=2)
             nc.tensor.transpose(gb_ps[:], gb_rows[:], ident_bf[:])
             nc.scalar.activation(out=half_gb[:], in_=gb_ps[:, 0 : C // P], func=ACT.Copy, scale=0.5)
 
-        def x_at(fn, name):
-            def go(k):
-                for i in XT[name].get(k, ()):
-                    fn(i)
-
-            return go
-
-        def gates(k):
-            for half, cb in GT.get(k, ()):
-                gate_mm(half, cb)
-                gate_tanh(half, cb)
-
-        def bias_next(n):
-            load_bias(n + 4)
-
-        def score_next(n):
-            scores(n + 1)
-
-        scale_spread()
-        x_mult(0, (0,))
+        x_cast(0, (0,), nc.vector.tensor_copy)
+        x_cast(0, (1,), nc.vector.tensor_copy)
         x_turn(0, (0,))
-        x_copy(0, (0,))
-        x_mult(0, (1,))
         x_turn(0, (1,))
-        x_quant(0, (0,))
-        scores(0)
-        x_copy(0, (1,))
-        x_mult(1)
-        x_quant(0, (1,))
+        x_cast(1, (0, 1), nc.vector.tensor_copy)
+        x_mult(0, (0,))
         x_turn(1)
-        x_copy(1)
         gain_spread(0, (0, 1, 2))
-        gain_spread(1, (0, 1, 2))
-
-        EARLY = 0
-        QL = 4
-        XT = {"mult": {0: (2,), 1: (3,), 3: (4,), 4: (5,), 5: (6,), 6: (7,)}, "turn": {0: (2,), 1: (3,), 3: (4,), 4: (5,), 5: (6,), 6: (7,)}, "quant": {0: (1,), 1: (2,), 2: (3,), 4: (4,), 5: (5,), 6: (6,), 7: (7,)}}
-        GT = {2: ((0, 0), (0, 1)), 3: ((0, 2), (0, 3)), 4: ((0, 4), (0, 5)), 5: ((0, 6), (0, 7)), 8: ((1, 0), (1, 1)), 9: ((1, 2), (1, 3)), 10: ((1, 4), (1, 5)), 11: ((1, 6), (1, 7))}
-        seq = (
-            (weigh, 5),
-            (norm, 5),
-            (turn, 3),
-            (turn_copy, 3),
-            (gate_turn, 5),
-            (add_a, 0),
-            (add_b, 0),
-            (shared_port(False), None),
-            (add_c, 0),
-            (bias_next, 0),
-            (score_next, 0),
-            (double, 1),
-            (x_at(x_turn, "turn"), None),
-            (x_at(x_copy, "turn"), None),
-            (inverse, 2),
-            (final, 6),
-            (row_max, 0),
-            (gates, None),
-            (expo, 0),
-            (gains, 0),
+        x_mult(0, (1,))
+        x_cast(2)
+        x_quant(0, (0,))
+        x_quant(0, (1,))
+        scores(0)
+        x_mult(1)
+        XC, XT, XM, XQ = (
+            {0: (3,), 1: (4,), 6: (5,), 7: (6,), 8: (7,)},
+            {0: (2,), 1: (3,), 3: (4,), 8: (5,), 9: (6,), 10: (7,)},
+            {1: (2,), 2: (3,), 3: (4,), 8: (5,), 9: (6,), 10: (7,)},
+            {1: (1,), 2: (2,), 3: (3,), 4: (4,), 9: (5,), 10: (6,), 11: (7,)},
         )
+        GT = {4: ((0, 0), (0, 1)), 5: ((0, 2), (0, 3)), 6: ((0, 4), (0, 5)), 7: ((0, 6), (0, 7)), 12: ((1, 0), (1, 1)), 13: ((1, 2), (1, 3)), 14: ((1, 4), (1, 5)), 15: ((1, 6), (1, 7))}
+        LAG_T, LAG_Q, LAG_W, LAG_G, LAG_F, LAG_V = 2, 3, 4, 6, 7, 2
+
+        def at(fn, n):
+            if 0 <= n < NT:
+                fn(n)
+
+        def at_x(fn, table, k):
+            for i in table.get(k, ()):
+                fn(i)
+
         for k in range(NT):
-            if k == 1:
+            at(weigh, k - LAG_W)
+            if k == 0:
+                gain_spread(1, (0, 1, 2))
+            add(k, (0, 1))
+            at(quant, k - LAG_Q)
+            for half, cb in GT.get(k, ()):
+                gate(half, cb)
+            at_x(x_quant, XQ, k)
+            add(k, (2,))
+            at_x(x_turn, XT, k)
+            at(norm, k - LAG_W)
+            if CUT < N and 0 <= k - LAG_V:
+                gains(k - LAG_V, CUT, N, nc.vector)
+            at_x(x_mult, XM, k)
+            if k == 3:
                 gb_prep()
-            for fn, lag in seq:
-                if k == LAST and fn is gates:
-                    break
-                if lag is None:
-                    fn(k)
-                elif 0 <= k - lag < NT:
-                    fn(k - lag)
-        gains_v(14)
-        turn(13)
-        turn_copy(13)
-        expo(15)
-        weigh(11)
-        gate_turn(11)
-        norm(11)
-        quant(12)
+            load_bias(k + 4)
+            scores(k + 1)
+            at_x(x_cast, XC, k)
+            at(gate_turn, k - LAG_G)
+            at(turn, k - LAG_T)
+            at(turn_copy, k - LAG_T)
+            at(final, k - LAG_F)
+            row_max(k)
+            expo(k)
+            if k % H == 1 and k > 1:
+                inverse(k // H - 1)
+            if k % H == 0 and k > 0:
+                double(k // H - 1)
+            if k < LAST:
+                gains(k, 0, CUT, nc.gpsimd)
+        final(9)
+        gate_turn(10)
         final(10)
-        gate_turn(12)
-        last_gains(0)
-        turn(14)
         weigh(12)
+        quant(13)
+        gate_turn(11)
+        gains(LAST, 0, 1024, nc.vector)
+        turn(14)
+        gains(LAST, 1024, 1536, nc.vector)
         turn_copy(14)
+        weigh(13)
+        gate_turn(12)
+        turn(15)
         norm(12)
         final(11)
-        last_gains(1)
-        gate_turn(13)
-        quant(13)
-        turn(15)
-        turn_copy(15)
-        weigh(13)
-        gate_turn(15)
-        final(12)
-        gate_turn(14)
-        inverse(14)
         quant(14)
+        double(7)
+        gate_turn(13)
         weigh(14)
+        turn_copy(15)
         norm(13)
-        double(15)
-        quant(15)
-        inverse(15)
+        final(12)
+        inverse(7)
         norm(14)
-        weigh(15)
+        quant(15)
+        if CUT < N:
+            gains(LAST - 1, CUT, N, nc.vector)
         final(13)
+        gate_turn(14)
         final(14)
+        weigh(15)
+        gate_turn(15)
         norm(15)
         final(15)

@@ -16,21 +16,41 @@ ACT = mybir.ActivationFunctionType
 AXIS = mybir.AxisListType
 
 P = 128
+PASS = 512
 M, N, H, D = 1024, 1536, 2, 512
 C = H * D
-IT = M // P
-NG = N // 512
-FLOPS = 2 * M * N * C * 2 + 2 * M * C * C
+GROUPS = M // P
+NG = N // PASS
+CB = C // P
+FLOPS = 2 * (2 * M * N * C + M * C * C)
 
-NT = H * IT
-LAST = NT - 1
-CUT = 1536
-LAST_PARTS = ((0, 1024), (1024, 1536))
-LAST_OUT = ((0, 256), (256, 512))
+STRIPS = GROUPS * H
+LAST = STRIPS - 1
+LAST_ANCHORS = ((0, 1024), (1024, N))
+LAST_OUT = ((0, 256), (256, D))
+
+LAG_TURN, LAG_QUANT, LAG_WEIGH, LAG_GATE_TURN, LAG_FINAL = 2, 3, 4, 6, 7
+X_CAST = {0: 3, 1: 4, 6: 5, 7: 6, 8: 7}
+X_TURN = {0: 2, 1: 3, 3: 4, 8: 5, 9: 6, 10: 7}
+X_SCALE = {1: 2, 2: 3, 3: 4, 8: 5, 9: 6, 10: 7}
+X_QUANT = {1: 1, 2: 2, 3: 3, 4: 4, 9: 5, 10: 6, 11: 7}
+GATE_START = (4, 12)
 
 
 def tile_relative_bias_anchor_attention_f1_kernel(
-    tc, x_bytes, x_scale, keys_words, keys_scales, rel_bias, anchor_gain, values_words, values_scales, gate_words, gate_scales, gate_bias, out
+    tc,
+    x_bytes,
+    x_scale,
+    keys_words,
+    keys_scales,
+    rel_bias,
+    anchor_gain,
+    values_words,
+    values_scales,
+    gate_words,
+    gate_scales,
+    gate_bias,
+    out,
 ):
     nc = tc.nc
     with ExitStack() as ctx:
@@ -39,380 +59,382 @@ def tile_relative_bias_anchor_attention_f1_kernel(
         psum = ctx.enter_context(tc.psum_pool(name="psum", bufs=1))
         ctx.enter_context(tc.manual_schedule())
 
+        def score_bank():
+            return psum.tile([P, PASS], F32, name="score_bank", bufs=3)
+
+        def turn_bank():
+            return psum.tile([P, 4, P], F32, name="turn_bank", bufs=2)
+
+        def gate_bank():
+            return psum.tile([P, 4, P], F32, name="gate_bank", bufs=2)
+
         scrap = keep.tile([P, 2], F32, name="scrap")
         nc.vector.memset(scrap[:, 0:1], 0.0)
         nc.scalar.activation(out=scrap[:, 1:2], in_=scrap[:, 0:1], func=ACT.Exp)
         ident = keep.tile([P, P], F32, name="ident")
         make_identity(nc, ident[:])
         ident_bf = keep.tile([P, P], BF16, name="ident_bf")
+        make_identity(nc, ident_bf[:])
 
-        x_raw = keep.tile([P, IT, C], U8, name="x_raw", align_bytes=64)
-        xs4 = keep.tile([P, H, 4], F32, name="xs4")
+        x_fp8 = keep.tile([P, GROUPS, C], U8, name="x_fp8", align_bytes=64)
+        x_factor = keep.tile([P, H, 4], F32, name="x_factor")
         keys_w = keep.tile([P, H, 2 * N], U8, name="keys_w", align_bytes=64)
-        vals_w = keep.tile([P, NG, 2 * C], U8, name="vals_w", align_bytes=64)
+        values_w = keep.tile([P, NG, 2 * C], U8, name="values_w", align_bytes=64)
         gate_w = keep.tile([P, H, 2 * C], U8, name="gate_w", align_bytes=64)
         keys_s = keep.tile([P, H, N], U8, name="keys_s", align_bytes=64)
-        vals_s = keep.tile([P, NG, C], U8, name="vals_s", align_bytes=64)
+        values_s = keep.tile([P, NG, C], U8, name="values_s", align_bytes=64)
         gate_s = keep.tile([P, H, C], U8, name="gate_s", align_bytes=64)
-        gain_b = keep.tile([P, H, N], BF16, name="gain_b")
-        gain_rows = keep.tile([P, H * N], BF16, name="gain_rows")
-        gb_rows = keep.tile([P, P], BF16, name="gb_rows")
-        half_gb = keep.tile([P, C // P], F32, name="half_gb")
+        gain = keep.tile([P, H, N], BF16, name="gain")
+        gain_row = keep.tile([P, H * N], BF16, name="gain_row")
         ones = keep.tile([P, P], BF16, name="ones")
+        gate_bias_rows = keep.tile([P, P], BF16, name="gate_bias_rows")
+        half_gate_bias = keep.tile([P, CB], F32, name="half_gate_bias")
         x_codes = keep.tile([P, H, M], U32, name="x_codes", align_bytes=64)
-        x_planes = keep.tile([P, H, M], U8, name="x_planes", align_bytes=64)
-        th = keep.tile([P, C // P, M], F32, name="th")
+        x_scales = keep.tile([P, H, M], U8, name="x_scales", align_bytes=64)
+        gate_tanh = keep.tile([P, CB, M], F32, name="gate_tanh")
 
-        nc.gpsimd.memset(gain_rows[:].bitcast(I32), 0)
-        for planes in (keys_s, vals_s, gate_s):
-            nc.vector.memset(planes[:].rearrange("p g n -> p (g n)").bitcast(I32), 0)
-        nc.vector.memset(gb_rows[:], 0.0)
+        nc.vector.memset(keys_s[:].rearrange("p g n -> p (g n)").bitcast(I32), 0)
+        nc.vector.memset(gain_row[:].bitcast(I32), 0)
+        nc.vector.memset(gate_bias_rows[:], 0.0)
         nc.vector.memset(ones[:], 1.0)
+        for scales in (values_s, gate_s):
+            nc.gpsimd.memset(scales[:].rearrange("p g n -> p (g n)").bitcast(I32), 0)
 
         x_rows = x_bytes.rearrange("(i p) c -> i p c", p=P)
-
-        def load_x(i):
-            nc.sync.dma_start(out=x_raw[:, i, :], in_=x_rows[i])
-
-        def load_words(tile, dram, g):
-            nc.sync.dma_start(out=tile[:, g, :].bitcast(I32), in_=dram[g].bitcast(I32))
-
-        def load_planes(tile, dram):
-            rows = dram.bitcast(I32).rearrange("g r n -> r g n")
-            for q in range(4):
-                nc.sync.dma_start(out=tile[32 * q : 32 * q + 4, :, :].bitcast(I32), in_=rows[4 * q : 4 * q + 4])
-
         bias = {}
 
-        def load_bias(n):
-            if n >= NT:
-                return
-            t = work.tile([P, N], BF16, name="bias", bufs=4)
-            bias[n] = t
-            i, h = n // H, n % H
-            nc.sync.dma_start(out=t[:], in_=rel_bias[h, i * P : (i + 1) * P, :])
+        def load_x(i):
+            nc.sync.dma_start(out=x_fp8[:, i, :], in_=x_rows[i])
 
-        nc.gpsimd.dma_start(out=gain_rows[0:1, :], in_=anchor_gain.rearrange("(o h) n -> o (h n)", o=1))
-        nc.gpsimd.dma_start(out=gb_rows[0 : C // P, :], in_=gate_bias.rearrange("(a b) -> a b", b=P))
+        def load_words(dst, src, g):
+            nc.sync.dma_start(out=dst[:, g, :].bitcast(I32), in_=src[g].bitcast(I32))
+
+        def load_scales(dst, src):
+            rows = src.bitcast(I32).rearrange("g r n -> r g n")
+            for q in range(4):
+                nc.sync.dma_start(out=dst[32 * q : 32 * q + 4, :, :].bitcast(I32), in_=rows[4 * q : 4 * q + 4])
+
+        def load_bias(n):
+            if n < STRIPS:
+                i, h = n // H, n % H
+                bias[n] = work.tile([P, N], BF16, name="bias", bufs=4)
+                nc.sync.dma_start(out=bias[n][:], in_=rel_bias[h, i * P : (i + 1) * P, :])
+
         load_x(0)
-        nc.sync.dma_start(out=xs4[:], in_=x_scale.rearrange("o (g p t) -> p (o g) t", p=P, t=4))
+        nc.sync.dma_start(out=x_factor[:], in_=x_scale.rearrange("o (g p t) -> p (o g) t", p=P, t=4))
         load_x(1)
-        load_planes(keys_s, keys_scales)
+        load_scales(keys_s, keys_scales)
         load_words(keys_w, keys_words, 0)
         load_bias(0)
+        nc.sync.dma_start(out=gain_row[0:1, :], in_=anchor_gain.rearrange("(o h) n -> o (h n)", o=1))
         load_x(2)
         load_words(keys_w, keys_words, 1)
         load_bias(1)
         load_x(3)
+        nc.sync.dma_start(out=gate_bias_rows[0:CB, :], in_=gate_bias.rearrange("(b p) -> b p", p=P))
         load_bias(2)
         load_x(4)
-        load_planes(vals_s, values_scales)
+        load_scales(values_s, values_scales)
         for g in range(NG):
-            load_words(vals_w, values_words, g)
-        load_planes(gate_s, gate_scales)
-        load_words(gate_w, gate_words, 0)
-        load_words(gate_w, gate_words, 1)
+            load_words(values_w, values_words, g)
+        load_scales(gate_s, gate_scales)
+        for g in range(H):
+            load_words(gate_w, gate_words, g)
         load_bias(3)
-        for i in range(5, IT):
+        for i in range(5, GROUPS):
             load_x(i)
 
-        make_identity(nc, ident_bf[:])
-
-        x_bf, x_ps, x_grp = {}, {}, {}
+        x_bf, x_turned, x_grouped = {}, {}, {}
 
         def x_cast(i, gs=(0, 1), copy=nc.scalar.copy):
             if i not in x_bf:
                 x_bf[i] = work.tile([P, C], BF16, name="x_bf", bufs=4)
-            s = slice(512 * gs[0], 512 * (gs[-1] + 1))
-            copy(out=x_bf[i][:, s], in_=x_raw[:, i, s].bitcast(FP8))
+            s = slice(PASS * gs[0], PASS * (gs[-1] + 1))
+            copy(out=x_bf[i][:, s], in_=x_fp8[:, i, s].bitcast(FP8))
 
         def x_turn(i, gs=(0, 1)):
             words = x_bf[i][:].bitcast(F32)
-            t = psum.tile([P, 4, P], F32, name="tr", bufs=2)
+            bank = turn_bank()
             for k, g in enumerate(gs):
-                x_ps[i, g] = t[:, 2 * k : 2 * k + 2, :]
+                x_turned[i, g] = bank[:, 2 * k : 2 * k + 2, :]
                 for u in range(2):
-                    nc.tensor.transpose(t[:, 2 * k + u, :], words[:, 256 * g + u : 256 * (g + 1) : 2], ident[:])
+                    nc.tensor.transpose(bank[:, 2 * k + u, :], words[:, 256 * g + u : 256 * (g + 1) : 2], ident[:])
 
-        def x_mult(i, gs=(0, 1)):
-            if i not in x_grp:
-                x_grp[i] = work.tile([P, H, P, 4], BF16, name="x_grp", bufs=3, align_bytes=64)
+        def x_scale_out(i, gs=(0, 1)):
+            if i not in x_grouped:
+                x_grouped[i] = work.tile([P, H, P, 4], BF16, name="x_grouped", bufs=3, align_bytes=64)
             for g in gs:
                 nc.vector.tensor_tensor(
-                    out=x_grp[i][:, g, :, :].rearrange("p r (u e) -> p r u e", e=2),
-                    in0=x_ps[i, g].bitcast(BF16).rearrange("p u (r e) -> p r u e", e=2),
-                    in1=xs4[:, g, :].unsqueeze(1).to_broadcast([P, P, 4]).rearrange("p r (u e) -> p r u e", e=2),
+                    out=x_grouped[i][:, g, :, :].rearrange("p r (u e) -> p r u e", e=2),
+                    in0=x_turned[i, g].bitcast(BF16).rearrange("p u (r e) -> p r u e", e=2),
+                    in1=x_factor[:, g, :].unsqueeze(1).to_broadcast([P, P, 4]).rearrange("p r (u e) -> p r u e", e=2),
                     op=ALU.mult,
                 )
 
         def x_quant(i, gs=(0, 1)):
+            s = slice(i * P, (i + 1) * P)
             for g in gs:
                 nc.vector.quantize_mx(
-                    out=x_codes[:, g, i * P : (i + 1) * P].bitcast(FP8X4),
-                    scales=x_planes[:, g, i * P : (i + 1) * P],
-                    in_=x_grp[i][:, g, :, :].rearrange("p r t -> p (r t)"),
+                    out=x_codes[:, g, s].bitcast(FP8X4),
+                    scales=x_scales[:, g, s],
+                    in_=x_grouped[i][:, g, :, :].rearrange("p r t -> p (r t)"),
                 )
 
-        def gain_spread(h, gs):
-            for g in gs:
-                t = psum.tile([P, 512], F32, name="sg", bufs=2)
-                nc.tensor.matmul(t[:], lhsT=ones[:], rhs=gain_rows[:, h * N + 512 * g : h * N + 512 * (g + 1)], start=True, stop=True)
+        def spread_gain(h):
+            for g in range(NG):
+                bank = psum.tile([P, PASS], F32, name="gate_bank", bufs=2)
+                first = h * N + PASS * g
+                nc.tensor.matmul(bank[:], lhsT=ones[:], rhs=gain_row[:, first : first + PASS], start=True, stop=True)
                 nc.scalar.copy(
-                    out=gain_b[:, h, 512 * g : 512 * (g + 1)].rearrange("p (u m e) -> p u m e", u=2, e=2),
-                    in_=t[:].rearrange("p (m u e) -> p u m e", u=2, e=2),
+                    out=gain[:, h, PASS * g : PASS * (g + 1)].rearrange("p (u m e) -> p u m e", u=2, e=2),
+                    in_=bank[:].rearrange("p (m u e) -> p u m e", u=2, e=2),
                 )
 
-        score = {}
+        def turn_gate_bias():
+            bank = psum.tile([P, P], BF16, name="gate_bank", bufs=2)
+            nc.tensor.transpose(bank[:], gate_bias_rows[:], ident_bf[:])
+            nc.scalar.activation(out=half_gate_bias[:], in_=bank[:, 0:CB], func=ACT.Copy, scale=0.5)
+
+        score, biased, minus_max, e_sum, e, u = {}, {}, {}, {}, {}, {}
+        u_turned, u_grouped, u_codes, u_scales = {}, {}, {}, {}
+        weighted, twice_sum, factor, normed, gate_turned = {}, {}, {}, {}, {}
 
         def scores(n):
-            if n >= NT:
+            if n >= STRIPS:
                 return
             i, h = n // H, n % H
+            s = slice(i * P, (i + 1) * P)
             for j in range(NG):
-                t = psum.tile([P, 512], F32, name="sc", bufs=3)
-                score[n, j] = t
+                score[n, j] = score_bank()
                 nc.tensor.matmul_mx(
-                    out=t[:],
-                    lhsT=x_codes[:, h, i * P : (i + 1) * P].bitcast(FP8X4),
-                    lhsT_scale=x_planes[:, h, i * P : (i + 1) * P],
-                    rhs=keys_w[:, h, 1024 * j : 1024 * (j + 1)].bitcast(FP4X4),
-                    rhs_scale=keys_s[:, h, 512 * j : 512 * (j + 1)],
+                    out=score[n, j][:],
+                    lhsT=x_codes[:, h, s].bitcast(FP8X4),
+                    lhsT_scale=x_scales[:, h, s],
+                    rhs=keys_w[:, h, 2 * PASS * j : 2 * PASS * (j + 1)].bitcast(FP4X4),
+                    rhs_scale=keys_s[:, h, PASS * j : PASS * (j + 1)],
                     start=True,
                     stop=True,
                 )
 
-        neg, nmax, esum, e_t, u_t, u_ps, grp, codes, planes_u, num, numr, rinv, twice, sg = ({} for _ in range(14))
-
-        def add(n, js):
-            if n not in neg:
-                neg[n] = work.tile([P, N], F32, name="neg", bufs=3)
+        def add_bias(n, js):
+            if n not in biased:
+                biased[n] = work.tile([P, N], F32, name="biased", bufs=3)
             for j in js:
-                s = slice(512 * j, 512 * (j + 1))
+                s = slice(PASS * j, PASS * (j + 1))
                 nc.vector.tensor_tensor(
-                    out=neg[n][:, s].rearrange("p (u m e) -> p u m e", u=2, e=2),
+                    out=biased[n][:, s].rearrange("p (u m e) -> p u m e", u=2, e=2),
                     in0=score[n, j][:].rearrange("p (m u e) -> p u m e", u=2, e=2),
                     in1=bias[n][:, s].rearrange("p (m u e) -> p u m e", u=2, e=2),
                     op=ALU.add,
                 )
 
         def row_max(n):
-            nmax[n] = work.tile([P, 1], F32, name="nmax", bufs=3)
-            nc.vector.tensor_reduce(out=nmax[n][:], in_=neg[n][:], axis=AXIS.X, op=ALU.max, negate=True)
+            minus_max[n] = work.tile([P, 1], F32, name="minus_max", bufs=3)
+            nc.vector.tensor_reduce(out=minus_max[n][:], in_=biased[n][:], axis=AXIS.X, op=ALU.max, negate=True)
 
-        def expo(n):
+        def exponential(n):
             i, h = n // H, n % H
-            e_t[n] = work.tile([P, N], F32, name="e_t", bufs=3)
+            e[n] = work.tile([P, N], F32, name="e", bufs=3)
             if h == 0:
-                esum[i] = work.tile([P, H + 1], F32, name="esum", bufs=4)
-            for k, (a, b) in enumerate(LAST_PARTS if n == LAST else ((0, N),)):
-                s = slice(a, b)
-                nc.scalar.activation(out=e_t[n][:, s], in_=neg[n][:, s], func=ACT.Exp, bias=nmax[n][:], scale=1.0, accum_out=esum[i][:, h + k : h + k + 1])
+                e_sum[i] = work.tile([P, H + 1], F32, name="e_sum", bufs=4)
+            for k, (a, b) in enumerate(LAST_ANCHORS if n == LAST else ((0, N),)):
+                nc.scalar.activation(
+                    out=e[n][:, a:b],
+                    in_=biased[n][:, a:b],
+                    func=ACT.Exp,
+                    bias=minus_max[n][:],
+                    scale=1.0,
+                    accum_out=e_sum[i][:, h + k : h + k + 1],
+                )
 
-        def gains(n, a, b, eng):
-            if n not in u_t:
-                u_t[n] = work.tile([P, N], BF16, name="u_t", bufs=5)
-            eng.tensor_tensor(out=u_t[n][:, a:b], in0=e_t[n][:, a:b], in1=gain_b[:, n % H, a:b], op=ALU.mult)
+        def apply_gain(n, a, b, engine):
+            if n not in u:
+                u[n] = work.tile([P, N], BF16, name="u", bufs=5)
+            engine.tensor_tensor(out=u[n][:, a:b], in0=e[n][:, a:b], in1=gain[:, n % H, a:b], op=ALU.mult)
 
         def turn(n):
-            words = u_t[n][:].bitcast(F32)
+            words = u[n][:].bitcast(F32)
             for part, gs in enumerate(((0, 1), (2,))):
-                t = psum.tile([P, 4, P], F32, name="tr", bufs=2)
-                u_ps[n, part] = t
+                bank = turn_bank()
+                u_turned[n, part] = bank
                 for k, g in enumerate(gs):
-                    for u in range(2):
-                        nc.tensor.transpose(t[:, 2 * k + u, :], words[:, 256 * g + P * u : 256 * g + P * (u + 1)], ident[:])
+                    for w in range(2):
+                        first = 256 * g + P * w
+                        nc.tensor.transpose(bank[:, 2 * k + w, :], words[:, first : first + P], ident[:])
 
         def turn_copy(n):
-            grp[n] = work.tile([P, NG, P, 4], BF16, name="grp", bufs=3, align_bytes=64)
+            u_grouped[n] = work.tile([P, NG, P, 4], BF16, name="u_grouped", bufs=3, align_bytes=64)
             for part, g0, ng in ((0, 0, 2), (1, 2, 1)):
-                dst = grp[n][:, g0 : g0 + ng, :, :].rearrange("p g r t -> p (g r t)").bitcast(F32)
+                words = u_grouped[n][:, g0 : g0 + ng, :, :].rearrange("p g r t -> p (g r t)").bitcast(F32)
                 nc.scalar.copy(
-                    out=dst.rearrange("p (g r u) -> p g r u", g=ng, u=2),
-                    in_=u_ps[n, part][:, 0 : 2 * ng, :].rearrange("p (g u) r -> p g r u", u=2),
+                    out=words.rearrange("p (g r w) -> p g r w", g=ng, w=2),
+                    in_=u_turned[n, part][:, 0 : 2 * ng, :].rearrange("p (g w) r -> p g r w", w=2),
                 )
 
         def quant(n):
-            codes[n] = work.tile([P, NG * P], U32, name="codes", bufs=4, align_bytes=64)
-            planes_u[n] = work.tile([P, NG * P], U8, name="planes_u", bufs=4, align_bytes=64)
+            u_codes[n] = work.tile([P, NG * P], U32, name="u_codes", bufs=4, align_bytes=64)
+            u_scales[n] = work.tile([P, NG * P], U8, name="u_scales", bufs=4, align_bytes=64)
             for g0, ng in ((0, 2), (2, 1)):
                 s = slice(g0 * P, (g0 + ng) * P)
                 nc.vector.quantize_mx(
-                    out=codes[n][:, s].bitcast(FP8X4),
-                    scales=planes_u[n][:, s],
-                    in_=grp[n][:, g0 : g0 + ng, :, :].rearrange("p g r t -> p (g r t)"),
+                    out=u_codes[n][:, s].bitcast(FP8X4),
+                    scales=u_scales[n][:, s],
+                    in_=u_grouped[n][:, g0 : g0 + ng, :, :].rearrange("p g r t -> p (g r t)"),
                 )
 
         def weigh(n):
             h = n % H
-            if n > NT - 4:
-                num[n] = psum.tile([P, 512], F32, name="sc", bufs=3)
-            else:
-                num[n] = psum.tile([P, 512], F32, name="num", bufs=1)
+            weighted[n] = score_bank() if n > LAST - 3 else psum.tile([P, D], F32, name="weighted", bufs=1)
             for g in range(NG):
                 s = slice(g * P, (g + 1) * P)
                 nc.tensor.matmul_mx(
-                    out=num[n][:],
-                    lhsT=codes[n][:, s].bitcast(FP8X4),
-                    lhsT_scale=planes_u[n][:, s],
-                    rhs=vals_w[:, g, 1024 * h : 1024 * (h + 1)].bitcast(FP4X4),
-                    rhs_scale=vals_s[:, g, 512 * h : 512 * (h + 1)],
+                    out=weighted[n][:],
+                    lhsT=u_codes[n][:, s].bitcast(FP8X4),
+                    lhsT_scale=u_scales[n][:, s],
+                    rhs=values_w[:, g, 2 * D * h : 2 * D * (h + 1)].bitcast(FP4X4),
+                    rhs_scale=values_s[:, g, D * h : D * (h + 1)],
                     start=(g == 0),
                     stop=(g == NG - 1),
                 )
 
-        def double(i):
-            if i == IT - 1:
-                nc.vector.tensor_tensor(out=esum[i][:, 1:2], in0=esum[i][:, 1:2], in1=esum[i][:, 2:3], op=ALU.add)
-            twice[i] = work.tile([P, H], F32, name="twice", bufs=5)
-            nc.scalar.activation(out=twice[i][:], in_=esum[i][:, 0:H], func=ACT.Copy, scale=2.0)
+        def double_sum(i):
+            if i == GROUPS - 1:
+                nc.vector.tensor_tensor(out=e_sum[i][:, 1:2], in0=e_sum[i][:, 1:2], in1=e_sum[i][:, 2:3], op=ALU.add)
+            twice_sum[i] = work.tile([P, H], F32, name="twice_sum", bufs=5)
+            nc.scalar.activation(out=twice_sum[i][:], in_=e_sum[i][:, 0:H], func=ACT.Copy, scale=2.0)
 
-        def inverse(i):
-            rinv[i] = work.tile([P, H], F32, name="rinv", bufs=7)
-            nc.vector.reciprocal(out=rinv[i][:], in_=twice[i][:])
+        def invert(i):
+            factor[i] = work.tile([P, H], F32, name="factor", bufs=7)
+            nc.vector.reciprocal(out=factor[i][:], in_=twice_sum[i][:])
 
         def norm(n):
             i, h = n // H, n % H
-            numr[n] = work.tile([P, 512], F32, name="numr", bufs=8)
-            for a, b in LAST_OUT if n == LAST else ((0, 512),):
-                nc.scalar.activation(out=numr[n][:, a:b], in_=num[n][:, a:b], func=ACT.Copy, scale=rinv[i][:, h : h + 1])
+            normed[n] = work.tile([P, D], F32, name="normed", bufs=8)
+            for a, b in LAST_OUT if n == LAST else ((0, D),):
+                nc.scalar.activation(out=normed[n][:, a:b], in_=weighted[n][:, a:b], func=ACT.Copy, scale=factor[i][:, h : h + 1])
 
-        def gate(half, cb):
-            z = psum.tile([P, 512], F32, name="tr", bufs=2)
-            s = slice(512 * half, 512 * (half + 1))
+        def gate(half, b):
+            bank = psum.tile([P, PASS], F32, name="turn_bank", bufs=2)
+            s = slice(PASS * half, PASS * (half + 1))
             for g in range(H):
                 nc.tensor.matmul_mx(
-                    out=z[:],
-                    lhsT=gate_w[:, g, 256 * cb : 256 * (cb + 1)].bitcast(FP4X4),
-                    lhsT_scale=gate_s[:, g, P * cb : P * (cb + 1)],
+                    out=bank[:],
+                    lhsT=gate_w[:, g, 2 * P * b : 2 * P * (b + 1)].bitcast(FP4X4),
+                    lhsT_scale=gate_s[:, g, P * b : P * (b + 1)],
                     rhs=x_codes[:, g, s].bitcast(FP8X4),
-                    rhs_scale=x_planes[:, g, s],
+                    rhs_scale=x_scales[:, g, s],
                     start=(g == 0),
                     stop=(g == H - 1),
                 )
-            nc.scalar.activation(out=th[:, cb, s], in_=z[:], func=ACT.Tanh, bias=half_gb[:, cb : cb + 1], scale=0.5)
+            nc.scalar.activation(
+                out=gate_tanh[:, b, s], in_=bank[:], func=ACT.Tanh, bias=half_gate_bias[:, b : b + 1], scale=0.5
+            )
 
         def gate_turn(n):
             i, h = n // H, n % H
-            if n == LAST:
-                sg[n] = psum.tile([P, 4, P], F32, name="tr", bufs=2)
-            else:
-                sg[n] = psum.tile([P, 4, P], F32, name="sg", bufs=2)
-            for q in range(4):
-                nc.tensor.transpose(sg[n][:, q, :], th[:, 4 * h + q, i * P : (i + 1) * P], ident[:])
+            gate_turned[n] = turn_bank() if n == LAST else gate_bank()
+            for b in range(4):
+                nc.tensor.transpose(gate_turned[n][:, b, :], gate_tanh[:, 4 * h + b, i * P : (i + 1) * P], ident[:])
 
         def final(n):
             i, h = n // H, n % H
-            for a, b in LAST_OUT if n == LAST else ((0, 512),):
-                o = work.tile([P, b - a], F32, name="o_t", bufs=4)
+            for a, b in LAST_OUT if n == LAST else ((0, D),):
+                result = work.tile([P, b - a], F32, name="result", bufs=4)
                 nc.vector.scalar_tensor_tensor(
-                    out=o[:],
-                    in0=sg[n][:].rearrange("p q r -> p (q r)")[:, a:b],
+                    out=result[:],
+                    in0=gate_turned[n][:].rearrange("p b r -> p (b r)")[:, a:b],
                     scalar=1.0,
-                    in1=numr[n][:, a:b],
+                    in1=normed[n][:, a:b],
                     op0=ALU.add,
                     op1=ALU.mult,
                 )
-                nc.sync.dma_start(out=out[i * P : (i + 1) * P, 512 * h + a : 512 * h + b], in_=o[:])
-
-        def gb_prep():
-            gb_ps = psum.tile([P, P], BF16, name="sg", bufs=2)
-            nc.tensor.transpose(gb_ps[:], gb_rows[:], ident_bf[:])
-            nc.scalar.activation(out=half_gb[:], in_=gb_ps[:, 0 : C // P], func=ACT.Copy, scale=0.5)
+                nc.sync.dma_start(out=out[i * P : (i + 1) * P, D * h + a : D * h + b], in_=result[:])
 
         x_cast(0, (0,), nc.vector.tensor_copy)
         x_cast(0, (1,), nc.vector.tensor_copy)
         x_turn(0, (0,))
+        x_cast(1, copy=nc.vector.tensor_copy)
+        x_scale_out(0, (0,))
         x_turn(0, (1,))
-        x_cast(1, (0, 1), nc.vector.tensor_copy)
-        x_mult(0, (0,))
         x_turn(1)
-        gain_spread(0, (0, 1, 2))
-        x_mult(0, (1,))
-        x_cast(2)
+        x_scale_out(0, (1,))
         x_quant(0, (0,))
-        x_quant(0, (1,))
         scores(0)
-        x_mult(1)
-        XC, XT, XM, XQ = (
-            {0: (3,), 1: (4,), 6: (5,), 7: (6,), 8: (7,)},
-            {0: (2,), 1: (3,), 3: (4,), 8: (5,), 9: (6,), 10: (7,)},
-            {1: (2,), 2: (3,), 3: (4,), 8: (5,), 9: (6,), 10: (7,)},
-            {1: (1,), 2: (2,), 3: (3,), 4: (4,), 9: (5,), 10: (6,), 11: (7,)},
-        )
-        GT = {4: ((0, 0), (0, 1)), 5: ((0, 2), (0, 3)), 6: ((0, 4), (0, 5)), 7: ((0, 6), (0, 7)), 12: ((1, 0), (1, 1)), 13: ((1, 2), (1, 3)), 14: ((1, 4), (1, 5)), 15: ((1, 6), (1, 7))}
-        LAG_T, LAG_Q, LAG_W, LAG_G, LAG_F, LAG_V = 2, 3, 4, 6, 7, 2
+        x_scale_out(1)
+        x_cast(2)
+        x_quant(0, (1,))
+        spread_gain(0)
 
-        def at(fn, n):
-            if 0 <= n < NT:
-                fn(n)
+        def strip(stage, n):
+            if 0 <= n < STRIPS:
+                stage(n)
 
-        def at_x(fn, table, k):
-            for i in table.get(k, ()):
-                fn(i)
+        def group(stage, steps, k):
+            if k in steps:
+                stage(steps[k])
 
-        for k in range(NT):
-            at(weigh, k - LAG_W)
-            if k == 0:
-                gain_spread(1, (0, 1, 2))
-            add(k, (0, 1))
-            at(quant, k - LAG_Q)
-            for half, cb in GT.get(k, ()):
-                gate(half, cb)
-            at_x(x_quant, XQ, k)
-            add(k, (2,))
-            at_x(x_turn, XT, k)
-            at(norm, k - LAG_W)
-            if CUT < N and 0 <= k - LAG_V:
-                gains(k - LAG_V, CUT, N, nc.vector)
-            at_x(x_mult, XM, k)
-            if k == 3:
-                gb_prep()
+        for k in range(STRIPS):
+            add_bias(k, (0, 1))
+            strip(quant, k - LAG_QUANT)
+            group(x_quant, X_QUANT, k)
+            if k == 1:
+                spread_gain(1)
+            add_bias(k, (2,))
+            strip(weigh, k - LAG_WEIGH)
+            strip(final, k - LAG_FINAL)
+            group(x_turn, X_TURN, k)
+            group(x_scale_out, X_SCALE, k)
+            for half, start in enumerate(GATE_START):
+                if start <= k < start + 4:
+                    gate(half, 2 * (k - start))
+                    gate(half, 2 * (k - start) + 1)
             load_bias(k + 4)
             scores(k + 1)
-            at_x(x_cast, XC, k)
-            at(gate_turn, k - LAG_G)
-            at(turn, k - LAG_T)
-            at(turn_copy, k - LAG_T)
-            at(final, k - LAG_F)
-            row_max(k)
-            expo(k)
-            if k % H == 1 and k > 1:
-                inverse(k // H - 1)
+            strip(norm, k - LAG_WEIGH)
+            strip(turn, k - LAG_TURN)
             if k % H == 0 and k > 0:
-                double(k // H - 1)
+                double_sum(k // H - 1)
+            row_max(k)
+            if k % H == 1 and k > 1:
+                invert(k // H - 1)
+            strip(turn_copy, k - LAG_TURN)
+            group(x_cast, X_CAST, k)
+            exponential(k)
             if k < LAST:
-                gains(k, 0, CUT, nc.gpsimd)
+                apply_gain(k, 0, N, nc.gpsimd)
+            if k == 3:
+                turn_gate_bias()
+            strip(gate_turn, k - LAG_GATE_TURN)
+
         final(9)
         gate_turn(10)
-        final(10)
         weigh(12)
-        quant(13)
+        final(10)
         gate_turn(11)
-        gains(LAST, 0, 1024, nc.vector)
-        turn(14)
-        gains(LAST, 1024, 1536, nc.vector)
-        turn_copy(14)
-        weigh(13)
+        quant(13)
         gate_turn(12)
-        turn(15)
+        turn(14)
         norm(12)
+        weigh(13)
+        for a, b in LAST_ANCHORS:
+            apply_gain(LAST, a, b, nc.vector)
         final(11)
-        quant(14)
-        double(7)
+        turn_copy(14)
+        turn(LAST)
         gate_turn(13)
-        weigh(14)
-        turn_copy(15)
+        quant(14)
         norm(13)
+        weigh(14)
         final(12)
-        inverse(7)
-        norm(14)
-        quant(15)
-        if CUT < N:
-            gains(LAST - 1, CUT, N, nc.vector)
-        final(13)
+        turn_copy(LAST)
+        double_sum(GROUPS - 1)
         gate_turn(14)
+        quant(LAST)
+        invert(GROUPS - 1)
+        final(13)
+        norm(14)
+        weigh(LAST)
+        norm(LAST)
+        gate_turn(LAST)
         final(14)
-        weigh(15)
-        gate_turn(15)
-        norm(15)
-        final(15)
+        final(LAST)

from contextlib import ExitStack

import concourse.mybir as mybir
from concourse.masks import make_identity

F32 = mybir.dt.float32
BF16 = mybir.dt.bfloat16
I32 = mybir.dt.int32
U32 = mybir.dt.uint32
U8 = mybir.dt.uint8
FP8 = mybir.dt.float8_e4m3fn
FP8X4 = mybir.dt.float8_e4m3fn_x4
FP4X4 = mybir.dt.float4_e2m1fn_x4
ALU = mybir.AluOpType
ACT = mybir.ActivationFunctionType
AXIS = mybir.AxisListType

P = 128
PASS = 512
M, N, H, D = 1024, 1536, 2, 512
C = H * D
GROUPS = M // P
NG = N // PASS
CB = C // P
FLOPS = 2 * (2 * M * N * C + M * C * C)

STRIPS = GROUPS * H
LAST = STRIPS - 1
LAST_ANCHORS = ((0, 1024), (1024, N))
LAST_OUT = ((0, 256), (256, D))

LAG_TURN, LAG_QUANT, LAG_WEIGH, LAG_GATE_TURN, LAG_FINAL = 2, 3, 4, 6, 7
X_CAST = {0: 3, 1: 4, 6: 5, 7: 6, 8: 7}
X_TURN = {0: 2, 1: 3, 3: 4, 8: 5, 9: 6, 10: 7}
X_SCALE = {1: 2, 2: 3, 3: 4, 8: 5, 9: 6, 10: 7}
X_QUANT = {1: 1, 2: 2, 3: 3, 4: 4, 9: 5, 10: 6, 11: 7}
GATE_START = (4, 12)


def tile_relative_bias_anchor_attention_f1_kernel(
    tc,
    x_bytes,
    x_scale,
    keys_words,
    keys_scales,
    rel_bias,
    anchor_gain,
    values_words,
    values_scales,
    gate_words,
    gate_scales,
    gate_bias,
    out,
):
    nc = tc.nc
    with ExitStack() as ctx:
        keep = ctx.enter_context(tc.tile_pool(name="keep", bufs=1))
        work = ctx.enter_context(tc.tile_pool(name="work", bufs=2))
        psum = ctx.enter_context(tc.psum_pool(name="psum", bufs=1))
        ctx.enter_context(tc.manual_schedule())

        def score_bank():
            return psum.tile([P, PASS], F32, name="score_bank", bufs=3)

        def turn_bank():
            return psum.tile([P, 4, P], F32, name="turn_bank", bufs=2)

        def gate_bank():
            return psum.tile([P, 4, P], F32, name="gate_bank", bufs=2)

        scrap = keep.tile([P, 2], F32, name="scrap")
        nc.vector.memset(scrap[:, 0:1], 0.0)
        nc.scalar.activation(out=scrap[:, 1:2], in_=scrap[:, 0:1], func=ACT.Exp)
        ident = keep.tile([P, P], F32, name="ident")
        make_identity(nc, ident[:])
        ident_bf = keep.tile([P, P], BF16, name="ident_bf")
        make_identity(nc, ident_bf[:])

        x_fp8 = keep.tile([P, GROUPS, C], U8, name="x_fp8", align_bytes=64)
        x_factor = keep.tile([P, H, 4], F32, name="x_factor")
        keys_w = keep.tile([P, H, 2 * N], U8, name="keys_w", align_bytes=64)
        values_w = keep.tile([P, NG, 2 * C], U8, name="values_w", align_bytes=64)
        gate_w = keep.tile([P, H, 2 * C], U8, name="gate_w", align_bytes=64)
        keys_s = keep.tile([P, H, N], U8, name="keys_s", align_bytes=64)
        values_s = keep.tile([P, NG, C], U8, name="values_s", align_bytes=64)
        gate_s = keep.tile([P, H, C], U8, name="gate_s", align_bytes=64)
        gain = keep.tile([P, H, N], BF16, name="gain")
        gain_row = keep.tile([P, H * N], BF16, name="gain_row")
        ones = keep.tile([P, P], BF16, name="ones")
        gate_bias_rows = keep.tile([P, P], BF16, name="gate_bias_rows")
        half_gate_bias = keep.tile([P, CB], F32, name="half_gate_bias")
        x_codes = keep.tile([P, H, M], U32, name="x_codes", align_bytes=64)
        x_scales = keep.tile([P, H, M], U8, name="x_scales", align_bytes=64)
        gate_tanh = keep.tile([P, CB, M], F32, name="gate_tanh")

        nc.vector.memset(keys_s[:].rearrange("p g n -> p (g n)").bitcast(I32), 0)
        nc.vector.memset(gain_row[:].bitcast(I32), 0)
        nc.vector.memset(gate_bias_rows[:], 0.0)
        nc.vector.memset(ones[:], 1.0)
        for scales in (values_s, gate_s):
            nc.gpsimd.memset(scales[:].rearrange("p g n -> p (g n)").bitcast(I32), 0)

        x_rows = x_bytes.rearrange("(i p) c -> i p c", p=P)
        bias = {}

        def load_x(i):
            nc.sync.dma_start(out=x_fp8[:, i, :], in_=x_rows[i])

        def load_words(dst, src, g):
            nc.sync.dma_start(out=dst[:, g, :].bitcast(I32), in_=src[g].bitcast(I32))

        def load_scales(dst, src):
            rows = src.bitcast(I32).rearrange("g r n -> r g n")
            for q in range(4):
                nc.sync.dma_start(out=dst[32 * q : 32 * q + 4, :, :].bitcast(I32), in_=rows[4 * q : 4 * q + 4])

        def load_bias(n):
            if n < STRIPS:
                i, h = n // H, n % H
                bias[n] = work.tile([P, N], BF16, name="bias", bufs=4)
                nc.sync.dma_start(out=bias[n][:], in_=rel_bias[h, i * P : (i + 1) * P, :])

        load_x(0)
        nc.sync.dma_start(out=x_factor[:], in_=x_scale.rearrange("o (g p t) -> p (o g) t", p=P, t=4))
        load_x(1)
        load_scales(keys_s, keys_scales)
        load_words(keys_w, keys_words, 0)
        load_bias(0)
        nc.sync.dma_start(out=gain_row[0:1, :], in_=anchor_gain.rearrange("(o h) n -> o (h n)", o=1))
        load_x(2)
        load_words(keys_w, keys_words, 1)
        load_bias(1)
        load_x(3)
        nc.sync.dma_start(out=gate_bias_rows[0:CB, :], in_=gate_bias.rearrange("(b p) -> b p", p=P))
        load_bias(2)
        load_x(4)
        load_scales(values_s, values_scales)
        for g in range(NG):
            load_words(values_w, values_words, g)
        load_scales(gate_s, gate_scales)
        for g in range(H):
            load_words(gate_w, gate_words, g)
        load_bias(3)
        for i in range(5, GROUPS):
            load_x(i)

        x_bf, x_turned, x_grouped = {}, {}, {}

        def x_cast(i, gs=(0, 1), copy=nc.scalar.copy):
            if i not in x_bf:
                x_bf[i] = work.tile([P, C], BF16, name="x_bf", bufs=4)
            s = slice(PASS * gs[0], PASS * (gs[-1] + 1))
            copy(out=x_bf[i][:, s], in_=x_fp8[:, i, s].bitcast(FP8))

        def x_turn(i, gs=(0, 1)):
            words = x_bf[i][:].bitcast(F32)
            bank = turn_bank()
            for k, g in enumerate(gs):
                x_turned[i, g] = bank[:, 2 * k : 2 * k + 2, :]
                for u in range(2):
                    nc.tensor.transpose(bank[:, 2 * k + u, :], words[:, 256 * g + u : 256 * (g + 1) : 2], ident[:])

        def x_scale_out(i, gs=(0, 1)):
            if i not in x_grouped:
                x_grouped[i] = work.tile([P, H, P, 4], BF16, name="x_grouped", bufs=3, align_bytes=64)
            for g in gs:
                nc.vector.tensor_tensor(
                    out=x_grouped[i][:, g, :, :].rearrange("p r (u e) -> p r u e", e=2),
                    in0=x_turned[i, g].bitcast(BF16).rearrange("p u (r e) -> p r u e", e=2),
                    in1=x_factor[:, g, :].unsqueeze(1).to_broadcast([P, P, 4]).rearrange("p r (u e) -> p r u e", e=2),
                    op=ALU.mult,
                )

        def x_quant(i, gs=(0, 1)):
            s = slice(i * P, (i + 1) * P)
            for g in gs:
                nc.vector.quantize_mx(
                    out=x_codes[:, g, s].bitcast(FP8X4),
                    scales=x_scales[:, g, s],
                    in_=x_grouped[i][:, g, :, :].rearrange("p r t -> p (r t)"),
                )

        def spread_gain(h):
            for g in range(NG):
                bank = psum.tile([P, PASS], F32, name="gate_bank", bufs=2)
                first = h * N + PASS * g
                nc.tensor.matmul(bank[:], lhsT=ones[:], rhs=gain_row[:, first : first + PASS], start=True, stop=True)
                nc.scalar.copy(
                    out=gain[:, h, PASS * g : PASS * (g + 1)].rearrange("p (u m e) -> p u m e", u=2, e=2),
                    in_=bank[:].rearrange("p (m u e) -> p u m e", u=2, e=2),
                )

        def turn_gate_bias():
            bank = psum.tile([P, P], BF16, name="gate_bank", bufs=2)
            nc.tensor.transpose(bank[:], gate_bias_rows[:], ident_bf[:])
            nc.scalar.activation(out=half_gate_bias[:], in_=bank[:, 0:CB], func=ACT.Copy, scale=0.5)

        score, biased, minus_max, e_sum, e, u = {}, {}, {}, {}, {}, {}
        u_turned, u_grouped, u_codes, u_scales = {}, {}, {}, {}
        weighted, twice_sum, factor, normed, gate_turned = {}, {}, {}, {}, {}

        def scores(n):
            if n >= STRIPS:
                return
            i, h = n // H, n % H
            s = slice(i * P, (i + 1) * P)
            for j in range(NG):
                score[n, j] = score_bank()
                nc.tensor.matmul_mx(
                    out=score[n, j][:],
                    lhsT=x_codes[:, h, s].bitcast(FP8X4),
                    lhsT_scale=x_scales[:, h, s],
                    rhs=keys_w[:, h, 2 * PASS * j : 2 * PASS * (j + 1)].bitcast(FP4X4),
                    rhs_scale=keys_s[:, h, PASS * j : PASS * (j + 1)],
                    start=True,
                    stop=True,
                )

        def add_bias(n, js):
            if n not in biased:
                biased[n] = work.tile([P, N], F32, name="biased", bufs=3)
            for j in js:
                s = slice(PASS * j, PASS * (j + 1))
                nc.vector.tensor_tensor(
                    out=biased[n][:, s].rearrange("p (u m e) -> p u m e", u=2, e=2),
                    in0=score[n, j][:].rearrange("p (m u e) -> p u m e", u=2, e=2),
                    in1=bias[n][:, s].rearrange("p (m u e) -> p u m e", u=2, e=2),
                    op=ALU.add,
                )

        def row_max(n):
            minus_max[n] = work.tile([P, 1], F32, name="minus_max", bufs=3)
            nc.vector.tensor_reduce(out=minus_max[n][:], in_=biased[n][:], axis=AXIS.X, op=ALU.max, negate=True)

        def exponential(n):
            i, h = n // H, n % H
            e[n] = work.tile([P, N], F32, name="e", bufs=3)
            if h == 0:
                e_sum[i] = work.tile([P, H + 1], F32, name="e_sum", bufs=4)
            for k, (a, b) in enumerate(LAST_ANCHORS if n == LAST else ((0, N),)):
                nc.scalar.activation(
                    out=e[n][:, a:b],
                    in_=biased[n][:, a:b],
                    func=ACT.Exp,
                    bias=minus_max[n][:],
                    scale=1.0,
                    accum_out=e_sum[i][:, h + k : h + k + 1],
                )

        def apply_gain(n, a, b, engine):
            if n not in u:
                u[n] = work.tile([P, N], BF16, name="u", bufs=5)
            engine.tensor_tensor(out=u[n][:, a:b], in0=e[n][:, a:b], in1=gain[:, n % H, a:b], op=ALU.mult)

        def turn(n):
            words = u[n][:].bitcast(F32)
            for part, gs in enumerate(((0, 1), (2,))):
                bank = turn_bank()
                u_turned[n, part] = bank
                for k, g in enumerate(gs):
                    for w in range(2):
                        first = 256 * g + P * w
                        nc.tensor.transpose(bank[:, 2 * k + w, :], words[:, first : first + P], ident[:])

        def turn_copy(n):
            u_grouped[n] = work.tile([P, NG, P, 4], BF16, name="u_grouped", bufs=3, align_bytes=64)
            for part, g0, ng in ((0, 0, 2), (1, 2, 1)):
                words = u_grouped[n][:, g0 : g0 + ng, :, :].rearrange("p g r t -> p (g r t)").bitcast(F32)
                nc.scalar.copy(
                    out=words.rearrange("p (g r w) -> p g r w", g=ng, w=2),
                    in_=u_turned[n, part][:, 0 : 2 * ng, :].rearrange("p (g w) r -> p g r w", w=2),
                )

        def quant(n):
            u_codes[n] = work.tile([P, NG * P], U32, name="u_codes", bufs=4, align_bytes=64)
            u_scales[n] = work.tile([P, NG * P], U8, name="u_scales", bufs=4, align_bytes=64)
            for g0, ng in ((0, 2), (2, 1)):
                s = slice(g0 * P, (g0 + ng) * P)
                nc.vector.quantize_mx(
                    out=u_codes[n][:, s].bitcast(FP8X4),
                    scales=u_scales[n][:, s],
                    in_=u_grouped[n][:, g0 : g0 + ng, :, :].rearrange("p g r t -> p (g r t)"),
                )

        def weigh(n):
            h = n % H
            weighted[n] = score_bank() if n > LAST - 3 else psum.tile([P, D], F32, name="weighted", bufs=1)
            for g in range(NG):
                s = slice(g * P, (g + 1) * P)
                nc.tensor.matmul_mx(
                    out=weighted[n][:],
                    lhsT=u_codes[n][:, s].bitcast(FP8X4),
                    lhsT_scale=u_scales[n][:, s],
                    rhs=values_w[:, g, 2 * D * h : 2 * D * (h + 1)].bitcast(FP4X4),
                    rhs_scale=values_s[:, g, D * h : D * (h + 1)],
                    start=(g == 0),
                    stop=(g == NG - 1),
                )

        def double_sum(i):
            if i == GROUPS - 1:
                nc.vector.tensor_tensor(out=e_sum[i][:, 1:2], in0=e_sum[i][:, 1:2], in1=e_sum[i][:, 2:3], op=ALU.add)
            twice_sum[i] = work.tile([P, H], F32, name="twice_sum", bufs=5)
            nc.scalar.activation(out=twice_sum[i][:], in_=e_sum[i][:, 0:H], func=ACT.Copy, scale=2.0)

        def invert(i):
            factor[i] = work.tile([P, H], F32, name="factor", bufs=7)
            nc.vector.reciprocal(out=factor[i][:], in_=twice_sum[i][:])

        def norm(n):
            i, h = n // H, n % H
            normed[n] = work.tile([P, D], F32, name="normed", bufs=8)
            for a, b in LAST_OUT if n == LAST else ((0, D),):
                nc.scalar.activation(out=normed[n][:, a:b], in_=weighted[n][:, a:b], func=ACT.Copy, scale=factor[i][:, h : h + 1])

        def gate(half, b):
            bank = psum.tile([P, PASS], F32, name="turn_bank", bufs=2)
            s = slice(PASS * half, PASS * (half + 1))
            for g in range(H):
                nc.tensor.matmul_mx(
                    out=bank[:],
                    lhsT=gate_w[:, g, 2 * P * b : 2 * P * (b + 1)].bitcast(FP4X4),
                    lhsT_scale=gate_s[:, g, P * b : P * (b + 1)],
                    rhs=x_codes[:, g, s].bitcast(FP8X4),
                    rhs_scale=x_scales[:, g, s],
                    start=(g == 0),
                    stop=(g == H - 1),
                )
            nc.scalar.activation(
                out=gate_tanh[:, b, s], in_=bank[:], func=ACT.Tanh, bias=half_gate_bias[:, b : b + 1], scale=0.5
            )

        def gate_turn(n):
            i, h = n // H, n % H
            gate_turned[n] = turn_bank() if n == LAST else gate_bank()
            for b in range(4):
                nc.tensor.transpose(gate_turned[n][:, b, :], gate_tanh[:, 4 * h + b, i * P : (i + 1) * P], ident[:])

        def final(n):
            i, h = n // H, n % H
            for a, b in LAST_OUT if n == LAST else ((0, D),):
                result = work.tile([P, b - a], F32, name="result", bufs=4)
                nc.vector.scalar_tensor_tensor(
                    out=result[:],
                    in0=gate_turned[n][:].rearrange("p b r -> p (b r)")[:, a:b],
                    scalar=1.0,
                    in1=normed[n][:, a:b],
                    op0=ALU.add,
                    op1=ALU.mult,
                )
                nc.sync.dma_start(out=out[i * P : (i + 1) * P, D * h + a : D * h + b], in_=result[:])

        x_cast(0, (0,), nc.vector.tensor_copy)
        x_cast(0, (1,), nc.vector.tensor_copy)
        x_turn(0, (0,))
        x_cast(1, copy=nc.vector.tensor_copy)
        x_scale_out(0, (0,))
        x_turn(0, (1,))
        x_turn(1)
        x_scale_out(0, (1,))
        x_quant(0, (0,))
        scores(0)
        x_scale_out(1)
        x_cast(2)
        x_quant(0, (1,))
        spread_gain(0)

        def strip(stage, n):
            if 0 <= n < STRIPS:
                stage(n)

        def group(stage, steps, k):
            if k in steps:
                stage(steps[k])

        for k in range(STRIPS):
            add_bias(k, (0, 1))
            strip(quant, k - LAG_QUANT)
            group(x_quant, X_QUANT, k)
            if k == 1:
                spread_gain(1)
            add_bias(k, (2,))
            strip(weigh, k - LAG_WEIGH)
            strip(final, k - LAG_FINAL)
            group(x_turn, X_TURN, k)
            group(x_scale_out, X_SCALE, k)
            for half, start in enumerate(GATE_START):
                if start <= k < start + 4:
                    gate(half, 2 * (k - start))
                    gate(half, 2 * (k - start) + 1)
            load_bias(k + 4)
            scores(k + 1)
            strip(norm, k - LAG_WEIGH)
            strip(turn, k - LAG_TURN)
            if k % H == 0 and k > 0:
                double_sum(k // H - 1)
            row_max(k)
            if k % H == 1 and k > 1:
                invert(k // H - 1)
            strip(turn_copy, k - LAG_TURN)
            group(x_cast, X_CAST, k)
            exponential(k)
            if k < LAST:
                apply_gain(k, 0, N, nc.gpsimd)
            if k == 3:
                turn_gate_bias()
            strip(gate_turn, k - LAG_GATE_TURN)

        final(9)
        gate_turn(10)
        weigh(12)
        final(10)
        gate_turn(11)
        quant(13)
        gate_turn(12)
        turn(14)
        norm(12)
        weigh(13)
        for a, b in LAST_ANCHORS:
            apply_gain(LAST, a, b, nc.vector)
        final(11)
        turn_copy(14)
        turn(LAST)
        gate_turn(13)
        quant(14)
        norm(13)
        weigh(14)
        final(12)
        turn_copy(LAST)
        double_sum(GROUPS - 1)
        gate_turn(14)
        quant(LAST)
        invert(GROUPS - 1)
        final(13)
        norm(14)
        weigh(LAST)
        norm(LAST)
        gate_turn(LAST)
        final(14)
        final(LAST)
